import numpy as np
import ml_dtypes


def mxq(x, axis, fmt="e4m3"):
    dtype, down = {"e4m3": (ml_dtypes.float8_e4m3fn, 7), "e5m2": (ml_dtypes.float8_e5m2, 14)}[fmt]
    v = np.moveaxis(np.asarray(x, np.float32).astype(ml_dtypes.bfloat16).astype(np.float64), axis, -1)
    blocks = v.reshape(v.shape[:-1] + (-1, 32))
    amax = np.abs(blocks).max(-1, keepdims=True)
    byte = np.maximum(np.where(amax > 0, np.frexp(amax)[1] - 1 + 127, 0) - down, 1)
    scale = np.exp2(byte - 127.0)
    codes = (blocks / scale).astype(np.float32).astype(dtype).astype(np.float64)
    return np.moveaxis((codes * scale).reshape(v.shape), -1, axis)


WIDE = False


def mx_kscale(k):
    if not WIDE:
        return np.ones(k)
    levels = np.array([10, -10, 5, -5, 0])
    if k % 512:
        return np.exp2(np.random.permutation(np.resize(levels, k // 32))).repeat(32)
    a = np.empty((k // 512, 16))
    for p in range(k // 512):
        a[p, :8] = np.random.permutation(np.resize(levels, 8))
        for g in range(8):
            far = levels[np.abs(levels - a[p, g]) >= 10]
            a[p, g + 8] = far[np.random.randint(len(far))]
    return np.exp2(a.ravel()).repeat(32)


def f64(x):
    return np.asarray(x).astype(np.float64)


def striped(idx):
    return np.tile(idx.reshape(-1, 16).T, (8, 1)).astype(np.uint16)


def unstriped(offs):
    return offs[:16].T.reshape(-1).astype(np.int64)


E2M1 = np.array([0.0, 0.5, 1.0, 1.5, 2.0, 3.0, 4.0, 6.0, -0.0, -0.5, -1.0, -1.5, -2.0, -3.0, -4.0, -6.0])


def pack_weight(w, fmt):
    k, n = w.shape
    w = f64(np.asarray(w, np.float32).astype(ml_dtypes.bfloat16)).reshape(k // 32, 32, n)
    amax = np.abs(w).max(1)
    if fmt == "e4m3":
        byte = np.frexp(amax)[1] - 1 + 127 - 7
    else:
        mant, ex = np.frexp(amax / 6.0)
        byte = np.where(mant > 0.5, ex, ex - 1) + 127
    byte = np.clip(np.where(amax > 0, byte, 1), 1, 254)
    scaled = (w * np.exp2(127.0 - byte)[:, None, :]).reshape(k, n).astype(np.float32)
    by_word = np.ascontiguousarray(scaled.reshape(k // 512, 128, 4, n).transpose(0, 1, 3, 2))
    if fmt == "e4m3":
        words = by_word.astype(ml_dtypes.float8_e4m3fn).view(np.uint8)
    else:
        c = by_word.astype(ml_dtypes.float4_e2m1fn).view(np.uint8) & 0xF
        words = (c[..., 0::2] | (c[..., 1::2] << 4)).reshape(k // 512, 128, 2 * n)
    return np.ascontiguousarray(words), np.ascontiguousarray(byte.astype(np.uint8).reshape(k // 512, 16, n))


def unpack_weight(words, scales, fmt):
    g, _, n = scales.shape
    words = np.ascontiguousarray(words).reshape(g, 128, n, -1)
    if fmt == "e4m3":
        vals = words.view(ml_dtypes.float8_e4m3fn).astype(np.float64)
    else:
        nib = np.empty((g, 128, n, 4), np.uint8)
        nib[..., 0::2] = words & 0xF
        nib[..., 1::2] = words >> 4
        vals = E2M1[nib]
    vals = vals * np.repeat(np.exp2(scales.astype(np.float64) - 127.0), 8, axis=1)[..., None]
    return vals.transpose(0, 1, 3, 2).reshape(g * 512, n)


def gelu(v):
    return 0.5 * v * (1.0 + np.tanh(np.sqrt(2.0 / np.pi) * (v + 0.044715 * v**3)))


K, T, E, C, H, N = 2048, 512, 8, 128, 512, 256


def by_expert(wq, xq):
    return np.concatenate([wq[e].T @ xq[:, e * C:(e + 1) * C] for e in range(E)], axis=1)


def setup_inputs():
    n = np.random.standard_normal
    s = mx_kscale(K)
    u = mx_kscale(H)
    first = np.random.permutation(np.repeat(np.arange(E), T // E))
    second = (first + 1 + np.random.permutation(np.repeat(np.arange(E - 1), -(-T // (E - 1)))[:T])) % E
    while np.bincount(second, minlength=E).max() != T // E:
        load = np.bincount(second, minlength=E); hi, lo = int(load.argmax()), int(load.argmin())
        t = np.flatnonzero((second == hi) & (first != lo))[0]; second[t] = lo
    slot_token = np.empty(E * C, np.int64); pos = np.empty((2, T), np.int64); fill = np.zeros(E, np.int64)
    place = np.stack([np.random.permutation(C) for _ in range(E)])
    for r, deal in enumerate((first, second)):
        for t in np.random.permutation(T):
            e = deal[t]; j = e * C + place[e, fill[e]]; fill[e] += 1; slot_token[j] = t; pos[r, t] = j
    g = np.random.uniform(0.2, 0.8, T)
    x = pack_weight(n((K, T)) * s[:, None], "e4m3")
    w = pack_weight(n((K, N)) / np.sqrt(K) / s[:, None], "e4m3")
    return {
        "x_words": x[0],
        "x_scales": x[1],
        "w_words": w[0],
        "w_scales": w[1],
        "wa": (n((E, K, H)) / np.sqrt(K) / s[None, :, None] * u).astype(np.float32),
        "wb": (n((E, H, N)) / np.sqrt(H) / u[None, :, None]).astype(np.float32),
        "gate": np.stack([np.tile(g, (128, 1)), np.tile(1.0 - g, (128, 1))]).astype(np.float32),
        "offs": striped(slot_token),
        "pos1": striped(pos[0]),
        "pos2": striped(pos[1]),
    }


def reference(x_words, x_scales, w_words, w_scales, wa, wb, gate, offs, pos1, pos2):
    w = unpack_weight(w_words, w_scales, "e4m3")
    waq = mxq(f64(wa), 1, "e4m3")
    wbq = mxq(f64(wb), 1, "e4m3")
    idx = unstriped(offs)
    x = unpack_weight(x_words, x_scales, "e4m3")
    base = w.T @ x
    h = gelu(by_expert(waq, x[:, idx]))
    y = by_expert(wbq, mxq(h, 0, "e4m3"))
    c = sum(f64(gate[r, :1]) * y[:, unstriped(p)] for r, p in enumerate((pos1, pos2)))
    return base + c

@@ -1,0 +1,186 @@
+from contextlib import ExitStack
+
+import concourse.mybir as mybir
+from concourse.masks import make_identity
+
+K, T, E, C, H, N = 2048, 512, 8, 128, 512, 256
+FLOPS = 2 * K * N * T + 2 * E * C * (K * H + H * N)
+
+F32 = mybir.dt.float32
+BF16 = mybir.dt.bfloat16
+I32 = mybir.dt.int32
+U32 = mybir.dt.uint32
+U16 = mybir.dt.uint16
+U8 = mybir.dt.uint8
+FP8X4 = mybir.dt.float8_e4m3fn_x4
+MULT = mybir.AluOpType.mult
+ADD = mybir.AluOpType.add
+GELU = mybir.ActivationFunctionType.Gelu_apprx_tanh
+
+P = 128
+PACK = 4
+K_PASS = P * PACK
+PASSES = K // K_PASS
+BLOCKS = N // P
+PAIR = 2 * C
+STREAM_BUFS = 12
+LAG = 3
+
+
+def tile_moe_adp_gelu_kernel(
+    tc, x_words, x_scales, w_words, w_scales, wa, wb, gate, offs, pos1, pos2, out
+):
+    nc = tc.nc
+    with ExitStack() as ctx:
+        keep = ctx.enter_context(tc.tile_pool(name="keep", bufs=1))
+        stream = ctx.enter_context(tc.tile_pool(name="stream", bufs=STREAM_BUFS))
+        work = ctx.enter_context(tc.tile_pool(name="work", bufs=4))
+        coded = ctx.enter_context(tc.tile_pool(name="coded", bufs=8))
+        psum = ctx.enter_context(tc.psum_pool(name="psum", bufs=2))
+        psum_y = ctx.enter_context(tc.psum_pool(name="psum_y", bufs=1))
+
+        offs_sb = keep.tile([P, E * C // 16], U16, name="offs_sb")
+        pos_sb = [keep.tile([P, T // 16], U16, name="pos%d_sb" % r) for r in range(2)]
+        x_sb = keep.tile([P, PASSES, T], I32, name="x_sb", align_bytes=64)
+        xs_sb = keep.tile([P, T], U8, name="xs_sb", align_bytes=64)
+        ws_sb = keep.tile([P, N], U8, name="ws_sb", align_bytes=64)
+        ident = keep.tile([P, P], F32, name="ident")
+        y_sb = [keep.tile([P, E * C], F32, name="y%d_sb" % b) for b in range(BLOCKS)]
+
+        nc.gpsimd.memset(xs_sb[:], 0)
+        nc.gpsimd.memset(ws_sb[:], 0)
+        make_identity(nc, ident[:])
+
+        def load_scale_rows(plane, scales, q):
+            nc.sync.dma_start(
+                out=plane[32 * q : 32 * q + 16, :].bitcast(I32),
+                in_=scales[:, 4 * q : 4 * q + 4, :].bitcast(I32),
+            )
+
+        nc.sync.dma_start(out=x_sb[:], in_=x_words.rearrange("s p t d -> p s (t d)").bitcast(I32))
+        nc.sync.dma_start(offs_sb[:], offs)
+        for q in range(4):
+            load_scale_rows(xs_sb, x_scales, q)
+
+        def gather_pair(g):
+            words = keep.tile([P, PASSES, PAIR], U32, name="xg%d" % g, align_bytes=64)
+            plane = keep.tile([P, PAIR], U8, name="xgs%d" % g, align_bytes=64)
+            entries = offs_sb[:, g * PAIR // 16 : (g + 1) * PAIR // 16]
+            nc.vector.tensor_copy(plane[:], xs_sb[:].indirect(entries))
+            for s in range(PASSES):
+                nc.vector.tensor_copy(words[:, s, :], x_sb[:, s, :].bitcast(U32).indirect(entries))
+            return words, plane
+
+        def load_rows(rows):
+            raw = stream.tile([P, PACK, rows.shape[1]], F32, name="raw", tag="stream", align_bytes=64)
+            nc.sync.dma_start(out=raw[:], in_=rows.rearrange("(p j) c -> p j c", j=PACK))
+            return raw
+
+        def interleave(copy, grouped, raw):
+            copy(
+                out=grouped.rearrange("p (c i) j -> p c j i", i=4),
+                in_=raw.rearrange("p j (c i) -> p c j i", i=4),
+            )
+
+        def quantize(grouped, label):
+            width = grouped.shape[1]
+            codes = coded.tile([P, width], U32, name=label + "_codes", align_bytes=64)
+            plane = coded.tile([P, width], U8, name=label + "_plane", align_bytes=64)
+            nc.vector.quantize_mx(
+                out=codes[:].bitcast(FP8X4),
+                scales=plane[:],
+                in_=grouped[:].rearrange("p c j -> p (c j)"),
+            )
+            return codes, plane
+
+        def first_layer(e, words, plane):
+            cols = slice((e % 2) * C, (e % 2 + 1) * C)
+            pre = psum.tile([C, H], F32, name="pre")
+            for s in range(PASSES):
+                raw = load_rows(wa[e, s * K_PASS : (s + 1) * K_PASS, :])
+                grouped = work.tile([P, H, PACK], BF16, name="a_grouped", align_bytes=64)
+                interleave(nc.vector.tensor_copy, grouped[:, : H // 2, :], raw[:, :, : H // 2])
+                interleave(nc.scalar.copy, grouped[:, H // 2 :, :], raw[:, :, H // 2 :])
+                a_codes, a_plane = quantize(grouped, "a")
+                nc.tensor.matmul_mx(
+                    out=pre[:],
+                    lhsT=words[:, s, cols].bitcast(FP8X4),
+                    lhsT_scale=plane[4 * s : P, cols],
+                    rhs=a_codes[:].bitcast(FP8X4),
+                    rhs_scale=a_plane[:],
+                    start=(s == 0),
+                    stop=(s == PASSES - 1),
+                )
+            h_rows = work.tile([C, 2, P, 2], BF16, name="h_rows", align_bytes=64)
+            nc.scalar.activation(
+                out=h_rows[:], in_=pre[:].rearrange("r (p u v) -> r u p v", u=2, v=2), func=GELU
+            )
+            h_pairs = h_rows[:].rearrange("r u p v -> r (u p v)").bitcast(F32)
+            turned = psum.tile([P, 2, C], F32, name="turned")
+            for u in range(2):
+                nc.tensor.transpose(turned[:, u, :], h_pairs[:, u * P : (u + 1) * P], ident[:])
+            h_grouped = work.tile([P, C, PACK], BF16, name="h_grouped", align_bytes=64)
+            nc.scalar.copy(out=h_grouped[:].bitcast(F32), in_=turned[:].rearrange("p u r -> p r u"))
+            return quantize(h_grouped, "h")
+
+        def second_layer(e, h_codes, h_plane):
+            raw = load_rows(wb[e])
+            for b, copy in enumerate((nc.vector.tensor_copy, nc.scalar.copy)):
+                grouped = work.tile([P, P, PACK], BF16, name="b%d_grouped" % b, align_bytes=64)
+                interleave(copy, grouped[:], raw[:, :, b * P : (b + 1) * P])
+                b_codes, b_plane = quantize(grouped, "b%d" % b)
+                y_ps = psum_y.tile([P, C], F32, name="y%d_ps" % b)
+                nc.tensor.matmul_mx(
+                    out=y_ps[:],
+                    lhsT=b_codes[:].bitcast(FP8X4),
+                    lhsT_scale=b_plane[:],
+                    rhs=h_codes[:].bitcast(FP8X4),
+                    rhs_scale=h_plane[:],
+                    start=True,
+                    stop=True,
+                )
+                nc.scalar.copy(out=y_sb[b][:, e * C : (e + 1) * C], in_=y_ps[:])
+
+        gathered = [gather_pair(0)]
+        hidden = []
+        for e in range(E):
+            hidden.append(first_layer(e, *gathered[e // 2]))
+            if e == 0:
+                for q in range(4):
+                    load_scale_rows(ws_sb, w_scales, q)
+            if e == 1:
+                nc.sync.dma_start(pos_sb[0][:], pos1)
+                nc.sync.dma_start(pos_sb[1][:], pos2)
+            if e % 2 == 0 and e + 2 < E:
+                gathered.append(gather_pair(e // 2 + 1))
+            if e >= LAG:
+                second_layer(e - LAG, *hidden[e - LAG])
+        for e in range(E - LAG, E):
+            second_layer(e, *hidden[e])
+
+        gate_sb = stream.tile([P, 2, T], F32, name="gate_sb", tag="stream", align_bytes=64)
+        nc.sync.dma_start(out=gate_sb[:], in_=gate.rearrange("r p t -> p r t"))
+        w_sb = stream.tile([P, PASSES, N], I32, name="w_sb", tag="stream", align_bytes=64)
+        nc.sync.dma_start(out=w_sb[:], in_=w_words.rearrange("s p n d -> p s (n d)").bitcast(I32))
+
+        for b in range(BLOCKS):
+            cols = slice(b * P, (b + 1) * P)
+            base = psum.tile([P, T], F32, name="base")
+            for s in range(PASSES):
+                nc.tensor.matmul_mx(
+                    out=base[:],
+                    lhsT=w_sb[:, s, cols].bitcast(FP8X4),
+                    lhsT_scale=ws_sb[4 * s : P, cols],
+                    rhs=x_sb[:, s, :].bitcast(FP8X4),
+                    rhs_scale=xs_sb[4 * s : P, :],
+                    start=(s == 0),
+                    stop=(s == PASSES - 1),
+                )
+            picked = [work.tile([P, T], F32, name="picked%d" % r) for r in range(2)]
+            for r in range(2):
+                nc.vector.tensor_tensor(picked[r][:], y_sb[b][:].indirect(pos_sb[r][:]), gate_sb[:, r, :], MULT)
+            partial = work.tile([P, T], F32, name="partial")
+            nc.vector.tensor_tensor(partial[:], picked[0][:], picked[1][:], ADD)
+            total = work.tile([P, T], F32, name="total")
+            nc.vector.tensor_tensor(total[:], partial[:], base[:], ADD)
+            nc.sync.dma_start(out=out[cols, :], in_=total[:])

@@ -23,8 +23,9 @@ K_PASS = P * PACK
 PASSES = K // K_PASS
 BLOCKS = N // P
 PAIR = 2 * C
-STREAM_BUFS = 12
+STREAM_BUFS = 14
 LAG = 3
+PER_BANK = 4
 
 
 def tile_moe_adp_gelu_kernel(
@@ -34,6 +35,7 @@ def tile_moe_adp_gelu_kernel(
     with ExitStack() as ctx:
         keep = ctx.enter_context(tc.tile_pool(name="keep", bufs=1))
         stream = ctx.enter_context(tc.tile_pool(name="stream", bufs=STREAM_BUFS))
+        twin = ctx.enter_context(tc.tile_pool(name="twin", bufs=2))
         work = ctx.enter_context(tc.tile_pool(name="work", bufs=4))
         coded = ctx.enter_context(tc.tile_pool(name="coded", bufs=8))
         psum = ctx.enter_context(tc.psum_pool(name="psum", bufs=2))
@@ -46,6 +48,10 @@ def tile_moe_adp_gelu_kernel(
         ws_sb = keep.tile([P, N], U8, name="ws_sb", align_bytes=64)
         ident = keep.tile([P, P], F32, name="ident")
         y_sb = [keep.tile([P, E * C], F32, name="y%d_sb" % b) for b in range(BLOCKS)]
+        y_ps = [
+            [psum_y.tile([P, PER_BANK * C], F32, name="y%d_%d_ps" % (b, a)) for a in range(E // PER_BANK)]
+            for b in range(BLOCKS)
+        ]
 
         nc.gpsimd.memset(xs_sb[:], 0)
         nc.gpsimd.memset(ws_sb[:], 0)
@@ -63,8 +69,8 @@ def tile_moe_adp_gelu_kernel(
             load_scale_rows(xs_sb, x_scales, q)
 
         def gather_pair(g):
-            words = keep.tile([P, PASSES, PAIR], U32, name="xg%d" % g, align_bytes=64)
-            plane = keep.tile([P, PAIR], U8, name="xgs%d" % g, align_bytes=64)
+            words = keep.tile([P, PASSES, PAIR], U32, name="slot_words%d" % g, align_bytes=64)
+            plane = keep.tile([P, PAIR], U8, name="slot_plane%d" % g, align_bytes=64)
             entries = offs_sb[:, g * PAIR // 16 : (g + 1) * PAIR // 16]
             nc.vector.tensor_copy(plane[:], xs_sb[:].indirect(entries))
             for s in range(PASSES):
@@ -82,26 +88,40 @@ def tile_moe_adp_gelu_kernel(
                 in_=raw.rearrange("p j (c i) -> p c j i", i=4),
             )
 
-        def quantize(grouped, label):
-            width = grouped.shape[1]
-            codes = coded.tile([P, width], U32, name=label + "_codes", align_bytes=64)
-            plane = coded.tile([P, width], U8, name=label + "_plane", align_bytes=64)
-            nc.vector.quantize_mx(
-                out=codes[:].bitcast(FP8X4),
-                scales=plane[:],
-                in_=grouped[:].rearrange("p c j -> p (c j)"),
-            )
+        def quantize(values, pool, label):
+            width = values.shape[1] // PACK
+            codes = pool.tile([P, width], U32, name=label + "_codes", align_bytes=64)
+            plane = pool.tile([P, width], U8, name=label + "_plane", align_bytes=64)
+            nc.vector.quantize_mx(out=codes[:].bitcast(FP8X4), scales=plane[:], in_=values)
             return codes, plane
 
-        def first_layer(e, words, plane):
+        def activate(pre, host):
+            pairs = host.rearrange("p j c -> p (j c)")[:, H // 2 : H]
+            nc.scalar.activation(
+                out=pairs.bitcast(BF16).rearrange("r (u p v) -> r u p v", u=2, v=2),
+                in_=pre[:].rearrange("r (p u v) -> r u p v", u=2, v=2),
+                func=GELU,
+            )
+            turned = psum.tile([P, 2, C], F32, name="turned")
+            for u in range(2):
+                nc.tensor.transpose(turned[:, u, :], pairs[:, u * P : (u + 1) * P], ident[:])
+            return turned
+
+        def quantize_hidden(turned, host):
+            pairs = host.rearrange("p j c -> p (j c)")[:, 2 * C : 4 * C]
+            nc.scalar.copy(out=pairs.rearrange("p (r u) -> p r u", u=2), in_=turned[:].rearrange("p u r -> p r u"))
+            return quantize(pairs.bitcast(BF16), coded, "h")
+
+        def first_layer(e, earlier):
+            words, plane = gathered[e // 2]
             cols = slice((e % 2) * C, (e % 2 + 1) * C)
-            pre = psum.tile([C, H], F32, name="pre")
+            pre = psum.tile([C, H], F32, name="pre", tag="sums")
             for s in range(PASSES):
                 raw = load_rows(wa[e, s * K_PASS : (s + 1) * K_PASS, :])
                 grouped = work.tile([P, H, PACK], BF16, name="a_grouped", align_bytes=64)
                 interleave(nc.vector.tensor_copy, grouped[:, : H // 2, :], raw[:, :, : H // 2])
                 interleave(nc.scalar.copy, grouped[:, H // 2 :, :], raw[:, :, H // 2 :])
-                a_codes, a_plane = quantize(grouped, "a")
+                a_codes, a_plane = quantize(grouped[:].rearrange("p c j -> p (c j)"), coded, "a")
                 nc.tensor.matmul_mx(
                     out=pre[:],
                     lhsT=words[:, s, cols].bitcast(FP8X4),
@@ -111,52 +131,60 @@ def tile_moe_adp_gelu_kernel(
                     start=(s == 0),
                     stop=(s == PASSES - 1),
                 )
-            h_rows = work.tile([C, 2, P, 2], BF16, name="h_rows", align_bytes=64)
-            nc.scalar.activation(
-                out=h_rows[:], in_=pre[:].rearrange("r (p u v) -> r u p v", u=2, v=2), func=GELU
-            )
-            h_pairs = h_rows[:].rearrange("r u p v -> r (u p v)").bitcast(F32)
-            turned = psum.tile([P, 2, C], F32, name="turned")
-            for u in range(2):
-                nc.tensor.transpose(turned[:, u, :], h_pairs[:, u * P : (u + 1) * P], ident[:])
-            h_grouped = work.tile([P, C, PACK], BF16, name="h_grouped", align_bytes=64)
-            nc.scalar.copy(out=h_grouped[:].bitcast(F32), in_=turned[:].rearrange("p u r -> p r u"))
-            return quantize(h_grouped, "h")
+                if e > 0 and s == 0:
+                    turned = activate(earlier, raw[:])
+                if e > 0 and s == 2:
+                    hidden.append(quantize_hidden(turned, raw[:]))
+            return pre
 
-        def second_layer(e, h_codes, h_plane):
+        def second_matrix(e):
             raw = load_rows(wb[e])
-            for b, copy in enumerate((nc.vector.tensor_copy, nc.scalar.copy)):
-                grouped = work.tile([P, P, PACK], BF16, name="b%d_grouped" % b, align_bytes=64)
-                interleave(copy, grouped[:], raw[:, :, b * P : (b + 1) * P])
-                b_codes, b_plane = quantize(grouped, "b%d" % b)
-                y_ps = psum_y.tile([P, C], F32, name="y%d_ps" % b)
+            grouped = work.tile([P, N, PACK], BF16, name="b_grouped", align_bytes=64)
+            interleave(nc.vector.tensor_copy, grouped[:, :P, :], raw[:, :, :P])
+            interleave(nc.scalar.copy, grouped[:, P:, :], raw[:, :, P:])
+            b_codes, b_plane = quantize(grouped[:].rearrange("p c j -> p (c j)"), work, "b")
+            return raw[:], b_codes, b_plane
+
+        def second_layer(e, b_codes, b_plane):
+            h_codes, h_plane = hidden[e]
+            bank, place = divmod(e, PER_BANK)
+            for b in range(BLOCKS):
+                cols = slice(b * P, (b + 1) * P)
                 nc.tensor.matmul_mx(
-                    out=y_ps[:],
-                    lhsT=b_codes[:].bitcast(FP8X4),
-                    lhsT_scale=b_plane[:],
+                    out=y_ps[b][bank][:, place * C : (place + 1) * C],
+                    lhsT=b_codes[:, cols].bitcast(FP8X4),
+                    lhsT_scale=b_plane[:, cols],
                     rhs=h_codes[:].bitcast(FP8X4),
                     rhs_scale=h_plane[:],
                     start=True,
                     stop=True,
                 )
-                nc.scalar.copy(out=y_sb[b][:, e * C : (e + 1) * C], in_=y_ps[:])
+            if place == PER_BANK - 1:
+                for b in range(BLOCKS):
+                    nc.scalar.copy(
+                        out=y_sb[b][:, bank * PER_BANK * C : (bank + 1) * PER_BANK * C], in_=y_ps[b][bank][:]
+                    )
 
-        gathered = [gather_pair(0)]
+        gathered = [gather_pair(g) for g in range(E // 2)]
         hidden = []
+        pre = None
         for e in range(E):
-            hidden.append(first_layer(e, *gathered[e // 2]))
+            pre = first_layer(e, pre)
             if e == 0:
                 for q in range(4):
                     load_scale_rows(ws_sb, w_scales, q)
             if e == 1:
                 nc.sync.dma_start(pos_sb[0][:], pos1)
                 nc.sync.dma_start(pos_sb[1][:], pos2)
-            if e % 2 == 0 and e + 2 < E:
-                gathered.append(gather_pair(e // 2 + 1))
             if e >= LAG:
-                second_layer(e - LAG, *hidden[e - LAG])
+                second_layer(e - LAG, *second_matrix(e - LAG)[1:])
         for e in range(E - LAG, E):
-            second_layer(e, *hidden[e])
+            raw, b_codes, b_plane = second_matrix(e)
+            if e == E - 3:
+                turned = activate(pre, raw)
+            if e == E - 1:
+                hidden.append(quantize_hidden(turned, raw))
+            second_layer(e, b_codes, b_plane)
 
         gate_sb = stream.tile([P, 2, T], F32, name="gate_sb", tag="stream", align_bytes=64)
         nc.sync.dma_start(out=gate_sb[:], in_=gate.rearrange("r p t -> p r t"))
@@ -165,7 +193,7 @@ def tile_moe_adp_gelu_kernel(
 
         for b in range(BLOCKS):
             cols = slice(b * P, (b + 1) * P)
-            base = psum.tile([P, T], F32, name="base")
+            base = psum.tile([P, T], F32, name="base", tag="sums")
             for s in range(PASSES):
                 nc.tensor.matmul_mx(
                     out=base[:],
@@ -176,11 +204,11 @@ def tile_moe_adp_gelu_kernel(
                     start=(s == 0),
                     stop=(s == PASSES - 1),
                 )
-            picked = [work.tile([P, T], F32, name="picked%d" % r) for r in range(2)]
+            picked = [twin.tile([P, T], F32, name="picked%d" % r) for r in range(2)]
             for r in range(2):
                 nc.vector.tensor_tensor(picked[r][:], y_sb[b][:].indirect(pos_sb[r][:]), gate_sb[:, r, :], MULT)
-            partial = work.tile([P, T], F32, name="partial")
+            partial = twin.tile([P, T], F32, name="partial")
             nc.vector.tensor_tensor(partial[:], picked[0][:], picked[1][:], ADD)
-            total = work.tile([P, T], F32, name="total")
+            total = twin.tile([P, T], F32, name="total")
             nc.vector.tensor_tensor(total[:], partial[:], base[:], ADD)
             nc.sync.dma_start(out=out[cols, :], in_=total[:])

@@ -23,7 +23,7 @@ K_PASS = P * PACK
 PASSES = K // K_PASS
 BLOCKS = N // P
 PAIR = 2 * C
-STREAM_BUFS = 14
+STREAM_BUFS = 8
 LAG = 3
 PER_BANK = 4
 
@@ -78,8 +78,12 @@ def tile_moe_adp_gelu_kernel(
             return words, plane
 
         def load_rows(rows):
-            raw = stream.tile([P, PACK, rows.shape[1]], F32, name="raw", tag="stream", align_bytes=64)
-            nc.sync.dma_start(out=raw[:], in_=rows.rearrange("(p j) c -> p j c", j=PACK))
+            passes = rows.shape[0] // K_PASS
+            raw = stream.tile([P, passes, PACK, rows.shape[1]], F32, name="raw", tag="stream", align_bytes=64)
+            nc.sync.dma_start(
+                out=raw[:].rearrange("p s j c -> p s (j c)"),
+                in_=rows.rearrange("(s p j) c -> p s (j c)", p=P, j=PACK),
+            )
             return raw
 
         def interleave(copy, grouped, raw):
@@ -116,8 +120,11 @@ def tile_moe_adp_gelu_kernel(
             words, plane = gathered[e // 2]
             cols = slice((e % 2) * C, (e % 2 + 1) * C)
             pre = psum.tile([C, H], F32, name="pre", tag="sums")
+            per_load = 1 if e >= E - 2 else 2
             for s in range(PASSES):
-                raw = load_rows(wa[e, s * K_PASS : (s + 1) * K_PASS, :])
+                if s % per_load == 0:
+                    loaded = load_rows(wa[e, s * K_PASS : (s + per_load) * K_PASS, :])
+                raw = loaded[:, s % per_load]
                 grouped = work.tile([P, H, PACK], BF16, name="a_grouped", align_bytes=64)
                 interleave(nc.vector.tensor_copy, grouped[:, : H // 2, :], raw[:, :, : H // 2])
                 interleave(nc.scalar.copy, grouped[:, H // 2 :, :], raw[:, :, H // 2 :])
@@ -132,18 +139,18 @@ def tile_moe_adp_gelu_kernel(
                     stop=(s == PASSES - 1),
                 )
                 if e > 0 and s == 0:
-                    turned = activate(earlier, raw[:])
+                    turned = activate(earlier, raw)
                 if e > 0 and s == 2:
-                    hidden.append(quantize_hidden(turned, raw[:]))
+                    hidden.append(quantize_hidden(turned, raw))
             return pre
 
         def second_matrix(e):
-            raw = load_rows(wb[e])
+            raw = load_rows(wb[e])[:, 0]
             grouped = work.tile([P, N, PACK], BF16, name="b_grouped", align_bytes=64)
             interleave(nc.vector.tensor_copy, grouped[:, :P, :], raw[:, :, :P])
             interleave(nc.scalar.copy, grouped[:, P:, :], raw[:, :, P:])
             b_codes, b_plane = quantize(grouped[:].rearrange("p c j -> p (c j)"), work, "b")
-            return raw[:], b_codes, b_plane
+            return raw, b_codes, b_plane
 
         def second_layer(e, b_codes, b_plane):
             h_codes, h_plane = hidden[e]

@@ -25,6 +25,7 @@ BLOCKS = N // P
 PAIR = 2 * C
 STREAM_BUFS = 8
 LAG = 3
+VECTOR_COLUMNS = 224
 PER_BANK = 4
 
 
@@ -120,14 +121,16 @@ def tile_moe_adp_gelu_kernel(
             words, plane = gathered[e // 2]
             cols = slice((e % 2) * C, (e % 2 + 1) * C)
             pre = psum.tile([C, H], F32, name="pre", tag="sums")
+            share = VECTOR_COLUMNS if e > 0 else 0
             per_load = 1 if e >= E - 2 else 2
             for s in range(PASSES):
                 if s % per_load == 0:
                     loaded = load_rows(wa[e, s * K_PASS : (s + per_load) * K_PASS, :])
                 raw = loaded[:, s % per_load]
                 grouped = work.tile([P, H, PACK], BF16, name="a_grouped", align_bytes=64)
-                interleave(nc.vector.tensor_copy, grouped[:, : H // 2, :], raw[:, :, : H // 2])
-                interleave(nc.scalar.copy, grouped[:, H // 2 :, :], raw[:, :, H // 2 :])
+                if share:
+                    interleave(nc.vector.tensor_copy, grouped[:, :share, :], raw[:, :, :share])
+                interleave(nc.scalar.copy, grouped[:, share:, :], raw[:, :, share:])
                 a_codes, a_plane = quantize(grouped[:].rearrange("p c j -> p (c j)"), coded, "a")
                 nc.tensor.matmul_mx(
                     out=pre[:],

@@ -16,17 +16,20 @@ FP8X4 = mybir.dt.float8_e4m3fn_x4
 MULT = mybir.AluOpType.mult
 ADD = mybir.AluOpType.add
 GELU = mybir.ActivationFunctionType.Gelu_apprx_tanh
+COPY = mybir.ActivationFunctionType.Copy
 
 P = 128
 PACK = 4
 K_PASS = P * PACK
 PASSES = K // K_PASS
 BLOCKS = N // P
+CHUNKS = T // P
 PAIR = 2 * C
-STREAM_BUFS = 8
+STREAM_BUFS = 16
 LAG = 3
-VECTOR_COLUMNS = 224
-PER_BANK = 4
+VECTOR_ROWS = 48
+VECTOR_ROWS_LATE = 72
+Y_GROUPS = ((0, 2), (2, 4), (4, 6), (6, 8))
 
 
 def tile_moe_adp_gelu_kernel(
@@ -48,15 +51,15 @@ def tile_moe_adp_gelu_kernel(
         xs_sb = keep.tile([P, T], U8, name="xs_sb", align_bytes=64)
         ws_sb = keep.tile([P, N], U8, name="ws_sb", align_bytes=64)
         ident = keep.tile([P, P], F32, name="ident")
+        gate1_sb = keep.tile([P, CHUNKS], F32, name="gate1_sb")
         y_sb = [keep.tile([P, E * C], F32, name="y%d_sb" % b) for b in range(BLOCKS)]
-        y_ps = [
-            [psum_y.tile([P, PER_BANK * C], F32, name="y%d_%d_ps" % (b, a)) for a in range(E // PER_BANK)]
-            for b in range(BLOCKS)
-        ]
 
         nc.gpsimd.memset(xs_sb[:], 0)
         nc.gpsimd.memset(ws_sb[:], 0)
         make_identity(nc, ident[:])
+
+        def bank(b, turn):
+            return psum_y.tile([P, CHUNKS, P], F32, name="bank", tag="bank%d_%d" % (b, turn % 2))
 
         def load_scale_rows(plane, scales, q):
             nc.sync.dma_start(
@@ -70,8 +73,8 @@ def tile_moe_adp_gelu_kernel(
             load_scale_rows(xs_sb, x_scales, q)
 
         def gather_pair(g):
-            words = keep.tile([P, PASSES, PAIR], U32, name="slot_words%d" % g, align_bytes=64)
-            plane = keep.tile([P, PAIR], U8, name="slot_plane%d" % g, align_bytes=64)
+            words = twin.tile([P, PASSES, PAIR], U32, name="slot_words", align_bytes=64)
+            plane = twin.tile([P, PAIR], U8, name="slot_plane", align_bytes=64)
             entries = offs_sb[:, g * PAIR // 16 : (g + 1) * PAIR // 16]
             nc.vector.tensor_copy(plane[:], xs_sb[:].indirect(entries))
             for s in range(PASSES):
@@ -79,19 +82,9 @@ def tile_moe_adp_gelu_kernel(
             return words, plane
 
         def load_rows(rows):
-            passes = rows.shape[0] // K_PASS
-            raw = stream.tile([P, passes, PACK, rows.shape[1]], F32, name="raw", tag="stream", align_bytes=64)
-            nc.sync.dma_start(
-                out=raw[:].rearrange("p s j c -> p s (j c)"),
-                in_=rows.rearrange("(s p j) c -> p s (j c)", p=P, j=PACK),
-            )
+            raw = stream.tile([P, PACK, rows.shape[1]], F32, name="raw", tag="stream", align_bytes=64)
+            nc.sync.dma_start(out=raw[:], in_=rows.rearrange("(p j) c -> p j c", j=PACK))
             return raw
-
-        def interleave(copy, grouped, raw):
-            copy(
-                out=grouped.rearrange("p (c i) j -> p c j i", i=4),
-                in_=raw.rearrange("p j (c i) -> p c j i", i=4),
-            )
 
         def quantize(values, pool, label):
             width = values.shape[1] // PACK
@@ -101,84 +94,79 @@ def tile_moe_adp_gelu_kernel(
             return codes, plane
 
         def activate(pre, host):
-            pairs = host.rearrange("p j c -> p (j c)")[:, H // 2 : H]
+            h = host.rearrange("p j c -> p (j c)")[:, H // 2 : H].bitcast(BF16)
             nc.scalar.activation(
-                out=pairs.bitcast(BF16).rearrange("r (u p v) -> r u p v", u=2, v=2),
-                in_=pre[:].rearrange("r (p u v) -> r u p v", u=2, v=2),
-                func=GELU,
+                out=h.rearrange("p (c t) -> p c t", t=PACK), in_=pre[:].rearrange("p t c -> p c t"), func=GELU
             )
-            turned = psum.tile([P, 2, C], F32, name="turned")
-            for u in range(2):
-                nc.tensor.transpose(turned[:, u, :], pairs[:, u * P : (u + 1) * P], ident[:])
-            return turned
-
-        def quantize_hidden(turned, host):
-            pairs = host.rearrange("p j c -> p (j c)")[:, 2 * C : 4 * C]
-            nc.scalar.copy(out=pairs.rearrange("p (r u) -> p r u", u=2), in_=turned[:].rearrange("p u r -> p r u"))
-            return quantize(pairs.bitcast(BF16), coded, "h")
+            hidden.append(quantize(h, coded, "h"))
 
         def first_layer(e, earlier):
             words, plane = gathered[e // 2]
             cols = slice((e % 2) * C, (e % 2 + 1) * C)
-            pre = psum.tile([C, H], F32, name="pre", tag="sums")
-            share = VECTOR_COLUMNS if e > 0 else 0
-            per_load = 1 if e >= E - 2 else 2
+            pre = psum.tile([P, PACK, C], F32, name="pre", tag="sums")
+            share = VECTOR_ROWS if e < E - 2 else VECTOR_ROWS_LATE
             for s in range(PASSES):
-                if s % per_load == 0:
-                    loaded = load_rows(wa[e, s * K_PASS : (s + per_load) * K_PASS, :])
-                raw = loaded[:, s % per_load]
-                grouped = work.tile([P, H, PACK], BF16, name="a_grouped", align_bytes=64)
-                if share:
-                    interleave(nc.vector.tensor_copy, grouped[:, :share, :], raw[:, :, :share])
-                interleave(nc.scalar.copy, grouped[:, share:, :], raw[:, :, share:])
-                a_codes, a_plane = quantize(grouped[:].rearrange("p c j -> p (c j)"), coded, "a")
-                nc.tensor.matmul_mx(
-                    out=pre[:],
-                    lhsT=words[:, s, cols].bitcast(FP8X4),
-                    lhsT_scale=plane[4 * s : P, cols],
-                    rhs=a_codes[:].bitcast(FP8X4),
-                    rhs_scale=a_plane[:],
-                    start=(s == 0),
-                    stop=(s == PASSES - 1),
-                )
+                raw = load_rows(wa[e, s * K_PASS : (s + 1) * K_PASS, :])
+                grouped = work.tile([P, PACK, P, PACK], BF16, name="a_grouped", align_bytes=64)
+                source = raw[:].rearrange("p j (m t) -> p m j t", t=PACK)
+                target = grouped[:].rearrange("p t m j -> p m j t")
+                nc.vector.tensor_copy(out=target[:, :share], in_=source[:, :share])
+                nc.scalar.copy(out=target[:, share:], in_=source[:, share:])
+                a_codes, a_plane = quantize(grouped[:].rearrange("p t m j -> p (t m j)"), coded, "a")
+                for t in range(PACK):
+                    nc.tensor.matmul_mx(
+                        out=pre[:, t, :],
+                        lhsT=a_codes[:, t * P : (t + 1) * P].bitcast(FP8X4),
+                        lhsT_scale=a_plane[:, t * P : (t + 1) * P],
+                        rhs=words[:, s, cols].bitcast(FP8X4),
+                        rhs_scale=plane[4 * s : P, cols],
+                        start=(s == 0 and t == 0),
+                        stop=(s == PASSES - 1 and t == PACK - 1),
+                    )
                 if e > 0 and s == 0:
-                    turned = activate(earlier, raw)
-                if e > 0 and s == 2:
-                    hidden.append(quantize_hidden(turned, raw))
+                    activate(earlier, raw[:])
             return pre
 
-        def second_matrix(e):
-            raw = load_rows(wb[e])[:, 0]
-            grouped = work.tile([P, N, PACK], BF16, name="b_grouped", align_bytes=64)
-            interleave(nc.vector.tensor_copy, grouped[:, :P, :], raw[:, :, :P])
-            interleave(nc.scalar.copy, grouped[:, P:, :], raw[:, :, P:])
-            b_codes, b_plane = quantize(grouped[:].rearrange("p c j -> p (c j)"), work, "b")
-            return raw, b_codes, b_plane
-
-        def second_layer(e, b_codes, b_plane):
+        def second_layer(e, earlier=None):
+            raw = load_rows(wb[e])
             h_codes, h_plane = hidden[e]
-            bank, place = divmod(e, PER_BANK)
+            turn = [a <= e < z for a, z in Y_GROUPS].index(True)
+            first, end = Y_GROUPS[turn]
             for b in range(BLOCKS):
-                cols = slice(b * P, (b + 1) * P)
+                grouped = work.tile([P, P, PACK], BF16, name="b_grouped", align_bytes=64)
+                copy = nc.vector.tensor_copy if b == 0 else nc.scalar.copy
+                copy(
+                    out=grouped[:].rearrange("p (c i) j -> p c j i", i=4),
+                    in_=raw[:, :, b * P : (b + 1) * P].rearrange("p j (c i) -> p c j i", i=4),
+                )
+                b_codes, b_plane = quantize(grouped[:].rearrange("p c j -> p (c j)"), work, "b")
+                if e == first:
+                    y_ps[b] = bank(b, turn)
                 nc.tensor.matmul_mx(
-                    out=y_ps[b][bank][:, place * C : (place + 1) * C],
-                    lhsT=b_codes[:, cols].bitcast(FP8X4),
-                    lhsT_scale=b_plane[:, cols],
+                    out=y_ps[b][:, e - first, :],
+                    lhsT=b_codes[:].bitcast(FP8X4),
+                    lhsT_scale=b_plane[:],
                     rhs=h_codes[:].bitcast(FP8X4),
                     rhs_scale=h_plane[:],
                     start=True,
                     stop=True,
                 )
-            if place == PER_BANK - 1:
-                for b in range(BLOCKS):
+                if e == end - 1:
                     nc.scalar.copy(
-                        out=y_sb[b][:, bank * PER_BANK * C : (bank + 1) * PER_BANK * C], in_=y_ps[b][bank][:]
+                        out=y_sb[b][:, first * C : end * C],
+                        in_=y_ps[b][:, : end - first, :].rearrange("p a c -> p (a c)"),
                     )
 
-        gathered = [gather_pair(g) for g in range(E // 2)]
+            if earlier is not None:
+                activate(earlier, raw[:])
+
+        gathered = []
         hidden = []
         pre = None
+        y_ps = [None] * BLOCKS
         for e in range(E):
+            if e % 2 == 0:
+                gathered.append(gather_pair(e // 2))
             pre = first_layer(e, pre)
             if e == 0:
                 for q in range(4):
@@ -186,39 +174,76 @@ def tile_moe_adp_gelu_kernel(
             if e == 1:
                 nc.sync.dma_start(pos_sb[0][:], pos1)
                 nc.sync.dma_start(pos_sb[1][:], pos2)
+                with nc.allow_non_contiguous_dma(reason="512 gate values, one token a partition"):
+                    nc.sync.dma_start(out=gate1_sb[:], in_=gate[0, 0, :].rearrange("(c p) -> p c", p=P))
             if e >= LAG:
-                second_layer(e - LAG, *second_matrix(e - LAG)[1:])
+                second_layer(e - LAG)
         for e in range(E - LAG, E):
-            raw, b_codes, b_plane = second_matrix(e)
-            if e == E - 3:
-                turned = activate(pre, raw)
-            if e == E - 1:
-                hidden.append(quantize_hidden(turned, raw))
-            second_layer(e, b_codes, b_plane)
+            second_layer(e, pre if e == E - LAG else None)
 
-        gate_sb = stream.tile([P, 2, T], F32, name="gate_sb", tag="stream", align_bytes=64)
-        nc.sync.dma_start(out=gate_sb[:], in_=gate.rearrange("r p t -> p r t"))
         w_sb = stream.tile([P, PASSES, N], I32, name="w_sb", tag="stream", align_bytes=64)
         nc.sync.dma_start(out=w_sb[:], in_=w_words.rearrange("s p n d -> p s (n d)").bitcast(I32))
 
-        for b in range(BLOCKS):
-            cols = slice(b * P, (b + 1) * P)
-            base = psum.tile([P, T], F32, name="base", tag="sums")
+        gate_sb = stream.tile([P, 2, T], F32, name="gate_sb", tag="stream", align_bytes=64)
+        nc.sync.dma_start(out=gate_sb[:], in_=gate.rearrange("r p t -> p r t"))
+        last_turn = len(Y_GROUPS) - 1
+        base_turned = bank(0, last_turn)
+        for c in range(CHUNKS):
+            tokens = slice(c * P, (c + 1) * P)
             for s in range(PASSES):
                 nc.tensor.matmul_mx(
-                    out=base[:],
-                    lhsT=w_sb[:, s, cols].bitcast(FP8X4),
-                    lhsT_scale=ws_sb[4 * s : P, cols],
-                    rhs=x_sb[:, s, :].bitcast(FP8X4),
-                    rhs_scale=xs_sb[4 * s : P, :],
+                    out=base_turned[:, c, :],
+                    lhsT=x_sb[:, s, tokens].bitcast(FP8X4),
+                    lhsT_scale=xs_sb[4 * s : P, tokens],
+                    rhs=w_sb[:, s, :P].bitcast(FP8X4),
+                    rhs_scale=ws_sb[4 * s : P, :P],
                     start=(s == 0),
                     stop=(s == PASSES - 1),
                 )
-            picked = [twin.tile([P, T], F32, name="picked%d" % r) for r in range(2)]
-            for r in range(2):
-                nc.vector.tensor_tensor(picked[r][:], y_sb[b][:].indirect(pos_sb[r][:]), gate_sb[:, r, :], MULT)
-            partial = twin.tile([P, T], F32, name="partial")
-            nc.vector.tensor_tensor(partial[:], picked[0][:], picked[1][:], ADD)
+        base_sb = keep.tile([P, CHUNKS, P], F32, name="base_sb")
+        nc.scalar.copy(out=base_sb[:], in_=base_turned[:])
+
+        plain = keep.tile([P, T], F32, name="plain")
+        nc.vector.tensor_copy(plain[:], y_sb[0][:].indirect(pos_sb[0][:]))
+        gated = {}
+        for b, r in ((1, 0), (1, 1), (0, 1)):
+            gated[b, r] = keep.tile([P, T], F32, name="gated%d_%d" % (b, r))
+            nc.vector.tensor_tensor(gated[b, r][:], y_sb[b][:].indirect(pos_sb[r][:]), gate_sb[:, r, :], MULT)
+
+        turned = psum.tile([P, CHUNKS, P], F32, name="turned", tag="sums")
+        scaled = keep.tile([P, CHUNKS, P], F32, name="scaled")
+        for c in range(CHUNKS):
+            nc.tensor.transpose(turned[:, c, :], plain[:, c * P : (c + 1) * P], ident[:])
+        for c in range(CHUNKS):
+            nc.scalar.activation(out=scaled[:, c, :], in_=turned[:, c, :], func=COPY, scale=gate1_sb[:, c : c + 1])
+
+        base = bank(1, last_turn)
+        for s in range(PASSES):
+            nc.tensor.matmul_mx(
+                out=base[:].rearrange("p c t -> p (c t)"),
+                lhsT=w_sb[:, s, P:].bitcast(FP8X4),
+                lhsT_scale=ws_sb[4 * s : P, P:],
+                rhs=x_sb[:, s, :].bitcast(FP8X4),
+                rhs_scale=xs_sb[4 * s : P, :],
+                start=(s == 0),
+                stop=(s == PASSES - 1),
+            )
+
+        partial = psum.tile([P, CHUNKS, P], F32, name="partial", tag="sums")
+        terms = [(term, c) for term in (base_sb, scaled) for c in range(CHUNKS)]
+        for place, (term, c) in enumerate(terms):
+            nc.tensor.matmul(
+                out=partial[:, c, :],
+                lhsT=term[:, c, :],
+                rhs=ident[:],
+                is_transpose=True,
+                start=(place == 0),
+                stop=(place == len(terms) - 1),
+            )
+
+        both = keep.tile([P, T], F32, name="both")
+        nc.vector.tensor_tensor(both[:], gated[1, 0][:], gated[1, 1][:], ADD)
+        for b, (left, right) in enumerate(((gated[0, 1], partial), (both, base))):
             total = twin.tile([P, T], F32, name="total")
-            nc.vector.tensor_tensor(total[:], partial[:], base[:], ADD)
-            nc.sync.dma_start(out=out[cols, :], in_=total[:])
+            nc.vector.tensor_tensor(total[:], left[:], right[:].rearrange("p c t -> p (c t)"), ADD)
+            nc.sync.dma_start(out=out[b * P : (b + 1) * P, :], in_=total[:])

@@ -25,11 +25,9 @@ PASSES = K // K_PASS
 BLOCKS = N // P
 CHUNKS = T // P
 PAIR = 2 * C
-STREAM_BUFS = 16
-LAG = 3
-VECTOR_ROWS = 48
-VECTOR_ROWS_LATE = 72
-Y_GROUPS = ((0, 2), (2, 4), (4, 6), (6, 8))
+STREAM_BUFS = 8
+LAG = 2
+PER_BANK = (2, 4)
 
 
 def tile_moe_adp_gelu_kernel(
@@ -40,8 +38,8 @@ def tile_moe_adp_gelu_kernel(
         keep = ctx.enter_context(tc.tile_pool(name="keep", bufs=1))
         stream = ctx.enter_context(tc.tile_pool(name="stream", bufs=STREAM_BUFS))
         twin = ctx.enter_context(tc.tile_pool(name="twin", bufs=2))
-        work = ctx.enter_context(tc.tile_pool(name="work", bufs=4))
-        coded = ctx.enter_context(tc.tile_pool(name="coded", bufs=8))
+        work = ctx.enter_context(tc.tile_pool(name="work", bufs=8))
+        coded = ctx.enter_context(tc.tile_pool(name="coded", bufs=16))
         psum = ctx.enter_context(tc.psum_pool(name="psum", bufs=2))
         psum_y = ctx.enter_context(tc.psum_pool(name="psum_y", bufs=1))
 
@@ -51,11 +49,14 @@ def tile_moe_adp_gelu_kernel(
         xs_sb = keep.tile([P, T], U8, name="xs_sb", align_bytes=64)
         ws_sb = keep.tile([P, N], U8, name="ws_sb", align_bytes=64)
         ident = keep.tile([P, P], F32, name="ident")
-        gate1_sb = keep.tile([P, CHUNKS], F32, name="gate1_sb")
+        gate_rows = keep.tile([P, P], F32, name="gate_rows")
+        gate_columns = keep.tile([P, 2 * CHUNKS], F32, name="gate_columns")
+        gate_sb = keep.tile([P, 2, T], F32, name="gate_sb")
         y_sb = [keep.tile([P, E * C], F32, name="y%d_sb" % b) for b in range(BLOCKS)]
 
         nc.gpsimd.memset(xs_sb[:], 0)
         nc.gpsimd.memset(ws_sb[:], 0)
+        nc.gpsimd.memset(gate_rows[:], 0.0)
         make_identity(nc, ident[:])
 
         def bank(b, turn):
@@ -82,8 +83,12 @@ def tile_moe_adp_gelu_kernel(
             return words, plane
 
         def load_rows(rows):
-            raw = stream.tile([P, PACK, rows.shape[1]], F32, name="raw", tag="stream", align_bytes=64)
-            nc.sync.dma_start(out=raw[:], in_=rows.rearrange("(p j) c -> p j c", j=PACK))
+            passes = rows.shape[0] // K_PASS
+            raw = stream.tile([P, passes, PACK, rows.shape[1]], F32, name="raw", tag="stream", align_bytes=64)
+            nc.sync.dma_start(
+                out=raw[:].rearrange("p s j c -> p s (j c)"),
+                in_=rows.rearrange("(s p j) c -> p s (j c)", p=P, j=PACK),
+            )
             return raw
 
         def quantize(values, pool, label):
@@ -104,35 +109,36 @@ def tile_moe_adp_gelu_kernel(
             words, plane = gathered[e // 2]
             cols = slice((e % 2) * C, (e % 2 + 1) * C)
             pre = psum.tile([P, PACK, C], F32, name="pre", tag="sums")
-            share = VECTOR_ROWS if e < E - 2 else VECTOR_ROWS_LATE
+            per_load = 2 if e < E - 2 else 1
             for s in range(PASSES):
-                raw = load_rows(wa[e, s * K_PASS : (s + 1) * K_PASS, :])
-                grouped = work.tile([P, PACK, P, PACK], BF16, name="a_grouped", align_bytes=64)
-                source = raw[:].rearrange("p j (m t) -> p m j t", t=PACK)
-                target = grouped[:].rearrange("p t m j -> p m j t")
-                nc.vector.tensor_copy(out=target[:, :share], in_=source[:, :share])
-                nc.scalar.copy(out=target[:, share:], in_=source[:, share:])
-                a_codes, a_plane = quantize(grouped[:].rearrange("p t m j -> p (t m j)"), coded, "a")
-                for t in range(PACK):
-                    nc.tensor.matmul_mx(
-                        out=pre[:, t, :],
-                        lhsT=a_codes[:, t * P : (t + 1) * P].bitcast(FP8X4),
-                        lhsT_scale=a_plane[:, t * P : (t + 1) * P],
-                        rhs=words[:, s, cols].bitcast(FP8X4),
-                        rhs_scale=plane[4 * s : P, cols],
-                        start=(s == 0 and t == 0),
-                        stop=(s == PASSES - 1 and t == PACK - 1),
-                    )
+                if s % per_load == 0:
+                    loaded = load_rows(wa[e, s * K_PASS : (s + per_load) * K_PASS, :])
+                raw = loaded[:, s % per_load]
+                source = raw.rearrange("p j (m u v) -> p u m j v", u=2, v=2)
+                for u, copy in enumerate((nc.vector.tensor_copy, nc.scalar.copy)):
+                    grouped = work.tile([P, 2, P, PACK], BF16, name="a_grouped", align_bytes=64)
+                    copy(out=grouped[:].rearrange("p v m j -> p m j v"), in_=source[:, u])
+                    a_codes, a_plane = quantize(grouped[:].rearrange("p v m j -> p (v m j)"), coded, "a")
+                    for v in range(2):
+                        nc.tensor.matmul_mx(
+                            out=pre[:, 2 * u + v, :],
+                            lhsT=a_codes[:, v * P : (v + 1) * P].bitcast(FP8X4),
+                            lhsT_scale=a_plane[:, v * P : (v + 1) * P],
+                            rhs=words[:, s, cols].bitcast(FP8X4),
+                            rhs_scale=plane[4 * s : P, cols],
+                            start=(s == 0 and u == 0 and v == 0),
+                            stop=(s == PASSES - 1 and u == 1 and v == 1),
+                        )
                 if e > 0 and s == 0:
-                    activate(earlier, raw[:])
+                    activate(earlier, raw)
             return pre
 
         def second_layer(e, earlier=None):
-            raw = load_rows(wb[e])
+            raw = load_rows(wb[e])[:, 0]
             h_codes, h_plane = hidden[e]
-            turn = [a <= e < z for a, z in Y_GROUPS].index(True)
-            first, end = Y_GROUPS[turn]
             for b in range(BLOCKS):
+                turn = e // PER_BANK[b]
+                first, end = turn * PER_BANK[b], (turn + 1) * PER_BANK[b]
                 grouped = work.tile([P, P, PACK], BF16, name="b_grouped", align_bytes=64)
                 copy = nc.vector.tensor_copy if b == 0 else nc.scalar.copy
                 copy(
@@ -158,7 +164,19 @@ def tile_moe_adp_gelu_kernel(
                     )
 
             if earlier is not None:
-                activate(earlier, raw[:])
+                activate(earlier, raw)
+
+        def spread_gates():
+            nc.sync.dma_start(out=gate_rows[: 2 * CHUNKS, :], in_=gate[:, 0, :].rearrange("r (c m) -> r c m", m=P))
+            upright = psum_y.tile([P, P], F32, name="upright", tag="spread")
+            nc.tensor.transpose(upright[:], gate_rows[:], ident[:])
+            nc.scalar.copy(out=gate_columns[:], in_=upright[:, : 2 * CHUNKS])
+            for r in range(2):
+                spread = psum_y.tile([P, CHUNKS, P], F32, name="spread", tag="spread")
+                for c in range(CHUNKS):
+                    column = gate_columns[:, r * CHUNKS + c : r * CHUNKS + c + 1]
+                    nc.tensor.transpose(spread[:, c, :], column.to_broadcast([P, P]), ident[:])
+                nc.scalar.copy(out=gate_sb[:, r, :], in_=spread[:].rearrange("p c t -> p (c t)"))
 
         gathered = []
         hidden = []
@@ -174,19 +192,16 @@ def tile_moe_adp_gelu_kernel(
             if e == 1:
                 nc.sync.dma_start(pos_sb[0][:], pos1)
                 nc.sync.dma_start(pos_sb[1][:], pos2)
-                with nc.allow_non_contiguous_dma(reason="512 gate values, one token a partition"):
-                    nc.sync.dma_start(out=gate1_sb[:], in_=gate[0, 0, :].rearrange("(c p) -> p c", p=P))
+                spread_gates()
             if e >= LAG:
-                second_layer(e - LAG)
+                second_layer(e - LAG, pre if e == E - 1 else None)
         for e in range(E - LAG, E):
-            second_layer(e, pre if e == E - LAG else None)
+            second_layer(e)
 
         w_sb = stream.tile([P, PASSES, N], I32, name="w_sb", tag="stream", align_bytes=64)
         nc.sync.dma_start(out=w_sb[:], in_=w_words.rearrange("s p n d -> p s (n d)").bitcast(I32))
 
-        gate_sb = stream.tile([P, 2, T], F32, name="gate_sb", tag="stream", align_bytes=64)
-        nc.sync.dma_start(out=gate_sb[:], in_=gate.rearrange("r p t -> p r t"))
-        last_turn = len(Y_GROUPS) - 1
+        last_turn = 1
         base_turned = bank(0, last_turn)
         for c in range(CHUNKS):
             tokens = slice(c * P, (c + 1) * P)
@@ -215,7 +230,7 @@ def tile_moe_adp_gelu_kernel(
         for c in range(CHUNKS):
             nc.tensor.transpose(turned[:, c, :], plain[:, c * P : (c + 1) * P], ident[:])
         for c in range(CHUNKS):
-            nc.scalar.activation(out=scaled[:, c, :], in_=turned[:, c, :], func=COPY, scale=gate1_sb[:, c : c + 1])
+            nc.scalar.activation(out=scaled[:, c, :], in_=turned[:, c, :], func=COPY, scale=gate_columns[:, c : c + 1])
 
         base = bank(1, last_turn)
         for s in range(PASSES):

@@ -201,8 +201,7 @@ def tile_moe_adp_gelu_kernel(
         w_sb = stream.tile([P, PASSES, N], I32, name="w_sb", tag="stream", align_bytes=64)
         nc.sync.dma_start(out=w_sb[:], in_=w_words.rearrange("s p n d -> p s (n d)").bitcast(I32))
 
-        last_turn = 1
-        base_turned = bank(0, last_turn)
+        base_turned = bank(0, 0)
         for c in range(CHUNKS):
             tokens = slice(c * P, (c + 1) * P)
             for s in range(PASSES):
@@ -232,7 +231,7 @@ def tile_moe_adp_gelu_kernel(
         for c in range(CHUNKS):
             nc.scalar.activation(out=scaled[:, c, :], in_=turned[:, c, :], func=COPY, scale=gate_columns[:, c : c + 1])
 
-        base = bank(1, last_turn)
+        base = bank(1, 0)
         for s in range(PASSES):
             nc.tensor.matmul_mx(
                 out=base[:].rearrange("p c t -> p (c t)"),
@@ -256,9 +255,17 @@ def tile_moe_adp_gelu_kernel(
                 stop=(place == len(terms) - 1),
             )
 
-        both = keep.tile([P, T], F32, name="both")
-        nc.vector.tensor_tensor(both[:], gated[1, 0][:], gated[1, 1][:], ADD)
-        for b, (left, right) in enumerate(((gated[0, 1], partial), (both, base))):
-            total = twin.tile([P, T], F32, name="total")
-            nc.vector.tensor_tensor(total[:], left[:], right[:].rearrange("p c t -> p (c t)"), ADD)
-            nc.sync.dma_start(out=out[b * P : (b + 1) * P, :], in_=total[:])
+        first = keep.tile([P, T], F32, name="first")
+        nc.vector.tensor_tensor(first[:], gated[0, 1][:], partial[:].rearrange("p c t -> p (c t)"), ADD)
+        nc.sync.dma_start(out=out[:P, :], in_=first[:])
+
+        both = gated[0, 1]
+        halves = [slice(half * T // 2, (half + 1) * T // 2) for half in range(2)]
+        for tokens in halves:
+            nc.vector.tensor_tensor(both[:, tokens], gated[1, 0][:, tokens], gated[1, 1][:, tokens], ADD)
+        for tokens in halves:
+            second = twin.tile([P, T // 2], F32, name="second")
+            nc.vector.tensor_tensor(
+                second[:], both[:, tokens], base[:].rearrange("p c t -> p (c t)")[:, tokens], ADD
+            )
+            nc.sync.dma_start(out=out[P:, tokens], in_=second[:])

@@ -16,7 +16,6 @@ FP8X4 = mybir.dt.float8_e4m3fn_x4
 MULT = mybir.AluOpType.mult
 ADD = mybir.AluOpType.add
 GELU = mybir.ActivationFunctionType.Gelu_apprx_tanh
-COPY = mybir.ActivationFunctionType.Copy
 
 P = 128
 PACK = 4
@@ -214,22 +213,8 @@ def tile_moe_adp_gelu_kernel(
                     start=(s == 0),
                     stop=(s == PASSES - 1),
                 )
-        base_sb = keep.tile([P, CHUNKS, P], F32, name="base_sb")
-        nc.scalar.copy(out=base_sb[:], in_=base_turned[:])
-
-        plain = keep.tile([P, T], F32, name="plain")
-        nc.vector.tensor_copy(plain[:], y_sb[0][:].indirect(pos_sb[0][:]))
-        gated = {}
-        for b, r in ((1, 0), (1, 1), (0, 1)):
-            gated[b, r] = keep.tile([P, T], F32, name="gated%d_%d" % (b, r))
-            nc.vector.tensor_tensor(gated[b, r][:], y_sb[b][:].indirect(pos_sb[r][:]), gate_sb[:, r, :], MULT)
-
-        turned = psum.tile([P, CHUNKS, P], F32, name="turned", tag="sums")
-        scaled = keep.tile([P, CHUNKS, P], F32, name="scaled")
-        for c in range(CHUNKS):
-            nc.tensor.transpose(turned[:, c, :], plain[:, c * P : (c + 1) * P], ident[:])
-        for c in range(CHUNKS):
-            nc.scalar.activation(out=scaled[:, c, :], in_=turned[:, c, :], func=COPY, scale=gate_columns[:, c : c + 1])
+        base_sb = keep.tile([P, T], F32, name="base_sb")
+        nc.scalar.copy(out=base_sb[:], in_=base_turned[:].rearrange("p c n -> p (c n)"))
 
         base = bank(1, 0)
         for s in range(PASSES):
@@ -243,26 +228,44 @@ def tile_moe_adp_gelu_kernel(
                 stop=(s == PASSES - 1),
             )
 
-        partial = psum.tile([P, CHUNKS, P], F32, name="partial", tag="sums")
-        terms = [(term, c) for term in (base_sb, scaled) for c in range(CHUNKS)]
-        for place, (term, c) in enumerate(terms):
-            nc.tensor.matmul(
-                out=partial[:, c, :],
-                lhsT=term[:, c, :],
-                rhs=ident[:],
-                is_transpose=True,
-                start=(place == 0),
-                stop=(place == len(terms) - 1),
-            )
-
-        first = keep.tile([P, T], F32, name="first")
-        nc.vector.tensor_tensor(first[:], gated[0, 1][:], partial[:].rearrange("p c t -> p (c t)"), ADD)
-        nc.sync.dma_start(out=out[:P, :], in_=first[:])
-
-        both = gated[0, 1]
         halves = [slice(half * T // 2, (half + 1) * T // 2) for half in range(2)]
+
+        def gated_choice(b, r, half=None):
+            tokens = slice(0, T) if half is None else halves[half]
+            width = tokens.stop - tokens.start
+            picked = keep.tile([P, width], F32, name="gated%d_%d_%d" % (b, r, tokens.start))
+            entries = pos_sb[r][:, tokens.start // 16 : tokens.stop // 16]
+            nc.vector.tensor_tensor(picked[:], y_sb[b][:].indirect(entries), gate_sb[:, r, tokens], MULT)
+            return picked[:]
+
+        def add_turned(terms, total, label):
+            steps = [(term, c) for term in terms for c in range(CHUNKS // 2)]
+            for place, (term, c) in enumerate(steps):
+                nc.tensor.matmul(
+                    out=total[:, c, :],
+                    lhsT=term[:, c * P : (c + 1) * P],
+                    rhs=ident[:],
+                    is_transpose=True,
+                    start=(place == 0),
+                    stop=(place == len(steps) - 1),
+                )
+            total_sb = keep.tile([P, T // 2], F32, name=label)
+            nc.scalar.copy(out=total_sb[:], in_=total[:, : CHUNKS // 2, :].rearrange("p c t -> p (c t)"))
+            return total_sb[:]
+
+        choice = gated_choice(0, 0)
+        routed = []
+        for half, tokens in enumerate(halves):
+            total = psum.tile([P, CHUNKS, P], F32, name="routed", tag="sums")
+            routed.append(add_turned((choice[:, tokens], gated_choice(0, 1, half)), total, "routed%d" % half))
+        for half, tokens in enumerate(halves):
+            result = add_turned((base_sb[:, tokens], routed[half]), bank(half, 1), "result%d" % half)
+            nc.scalar.dma_start(out=out[:P, tokens], in_=result)
+
+        choices = [gated_choice(1, r) for r in range(2)]
+        both = keep.tile([P, T], F32, name="both")
         for tokens in halves:
-            nc.vector.tensor_tensor(both[:, tokens], gated[1, 0][:, tokens], gated[1, 1][:, tokens], ADD)
+            nc.vector.tensor_tensor(both[:, tokens], choices[0][:, tokens], choices[1][:, tokens], ADD)
         for tokens in halves:
             second = twin.tile([P, T // 2], F32, name="second")
             nc.vector.tensor_tensor(

@@ -132,38 +132,37 @@ def tile_moe_adp_gelu_kernel(
                     activate(earlier, raw)
             return pre
 
-        def second_layer(e, earlier=None):
-            raw = load_rows(wb[e])[:, 0]
+        def second_layer(e, b, raw, copy):
             h_codes, h_plane = hidden[e]
-            for b in range(BLOCKS):
-                turn = e // PER_BANK[b]
-                first, end = turn * PER_BANK[b], (turn + 1) * PER_BANK[b]
-                grouped = work.tile([P, P, PACK], BF16, name="b_grouped", align_bytes=64)
-                copy = nc.vector.tensor_copy if b == 0 else nc.scalar.copy
-                copy(
-                    out=grouped[:].rearrange("p (c i) j -> p c j i", i=4),
-                    in_=raw[:, :, b * P : (b + 1) * P].rearrange("p j (c i) -> p c j i", i=4),
+            turn, place = divmod(e, PER_BANK[b])
+            grouped = work.tile([P, P, PACK], BF16, name="b_grouped", align_bytes=64)
+            copy(
+                out=grouped[:].rearrange("p (c i) j -> p c j i", i=4),
+                in_=raw.rearrange("p j (c i) -> p c j i", i=4),
+            )
+            b_codes, b_plane = quantize(grouped[:].rearrange("p c j -> p (c j)"), work, "b")
+            if place == 0:
+                y_ps[b] = bank(b, turn)
+            nc.tensor.matmul_mx(
+                out=y_ps[b][:, place, :],
+                lhsT=b_codes[:].bitcast(FP8X4),
+                lhsT_scale=b_plane[:],
+                rhs=h_codes[:].bitcast(FP8X4),
+                rhs_scale=h_plane[:],
+                start=True,
+                stop=True,
+            )
+            if place == PER_BANK[b] - 1:
+                nc.scalar.copy(
+                    out=y_sb[b][:, turn * PER_BANK[b] * C : (e + 1) * C],
+                    in_=y_ps[b][:, : PER_BANK[b], :].rearrange("p a c -> p (a c)"),
                 )
-                b_codes, b_plane = quantize(grouped[:].rearrange("p c j -> p (c j)"), work, "b")
-                if e == first:
-                    y_ps[b] = bank(b, turn)
-                nc.tensor.matmul_mx(
-                    out=y_ps[b][:, e - first, :],
-                    lhsT=b_codes[:].bitcast(FP8X4),
-                    lhsT_scale=b_plane[:],
-                    rhs=h_codes[:].bitcast(FP8X4),
-                    rhs_scale=h_plane[:],
-                    start=True,
-                    stop=True,
-                )
-                if e == end - 1:
-                    nc.scalar.copy(
-                        out=y_sb[b][:, first * C : end * C],
-                        in_=y_ps[b][:, : end - first, :].rearrange("p a c -> p (a c)"),
-                    )
 
-            if earlier is not None:
-                activate(earlier, raw)
+        def second_layer_whole(e):
+            raw = load_rows(wb[e])[:, 0]
+            second_layer(e, 0, raw[:, :, :P], nc.vector.tensor_copy)
+            second_layer(e, 1, raw[:, :, P:], nc.scalar.copy)
+            return raw
 
         def spread_gates():
             nc.sync.dma_start(out=gate_rows[: 2 * CHUNKS, :], in_=gate[:, 0, :].rearrange("r (c m) -> r c m", m=P))
@@ -193,9 +192,13 @@ def tile_moe_adp_gelu_kernel(
                 nc.sync.dma_start(pos_sb[1][:], pos2)
                 spread_gates()
             if e >= LAG:
-                second_layer(e - LAG, pre if e == E - 1 else None)
-        for e in range(E - LAG, E):
-            second_layer(e)
+                spent = second_layer_whole(e - LAG)
+        activate(pre, spent)
+        for b in range(BLOCKS):
+            for e in range(E - LAG, E):
+                raw = stream.tile([P, PACK, P], F32, name="half", tag="stream", align_bytes=64)
+                nc.sync.dma_start(out=raw[:], in_=wb[e, :, b * P : (b + 1) * P].rearrange("(p j) c -> p j c", j=PACK))
+                second_layer(e, b, raw[:], nc.vector.tensor_copy if e == E - 1 else nc.scalar.copy)
 
         w_sb = stream.tile([P, PASSES, N], I32, name="w_sb", tag="stream", align_bytes=64)
         nc.sync.dma_start(out=w_sb[:], in_=w_words.rearrange("s p n d -> p s (n d)").bitcast(I32))

@@ -54,15 +54,12 @@ def tile_moe_adp_gelu_kernel(
         y_sb = [keep.tile([P, E * C], F32, name="y%d_sb" % b) for b in range(BLOCKS)]
 
         nc.gpsimd.memset(xs_sb[:], 0)
-        nc.gpsimd.memset(ws_sb[:], 0)
-        nc.gpsimd.memset(gate_rows[:], 0.0)
-        make_identity(nc, ident[:])
 
         def bank(b, turn):
             return psum_y.tile([P, CHUNKS, P], F32, name="bank", tag="bank%d_%d" % (b, turn % 2))
 
         def load_scale_rows(plane, scales, q):
-            nc.sync.dma_start(
+            nc.gpsimd.dma_start(
                 out=plane[32 * q : 32 * q + 16, :].bitcast(I32),
                 in_=scales[:, 4 * q : 4 * q + 4, :].bitcast(I32),
             )
@@ -71,6 +68,9 @@ def tile_moe_adp_gelu_kernel(
         nc.sync.dma_start(offs_sb[:], offs)
         for q in range(4):
             load_scale_rows(xs_sb, x_scales, q)
+        nc.gpsimd.memset(gate_rows[:], 0.0)
+        make_identity(nc, ident[:])
+        nc.gpsimd.memset(ws_sb[:], 0)
 
         def gather_pair(g):
             words = twin.tile([P, PASSES, PAIR], U32, name="slot_words", align_bytes=64)

@@ -44,7 +44,7 @@ def tile_moe_adp_gelu_kernel(
 
         offs_sb = keep.tile([P, E * C // 16], U16, name="offs_sb")
         pos_sb = [keep.tile([P, T // 16], U16, name="pos%d_sb" % r) for r in range(2)]
-        x_sb = keep.tile([P, PASSES, T], I32, name="x_sb", align_bytes=64)
+        x_sb = keep.tile([P, PASSES, T], I32, name="x_sb", align_bytes=256)
         xs_sb = keep.tile([P, T], U8, name="xs_sb", align_bytes=64)
         ws_sb = keep.tile([P, N], U8, name="ws_sb", align_bytes=64)
         ident = keep.tile([P, P], F32, name="ident")
@@ -83,7 +83,7 @@ def tile_moe_adp_gelu_kernel(
 
         def load_rows(rows):
             passes = rows.shape[0] // K_PASS
-            raw = stream.tile([P, passes, PACK, rows.shape[1]], F32, name="raw", tag="stream", align_bytes=64)
+            raw = stream.tile([P, passes, PACK, rows.shape[1]], F32, name="raw", tag="stream", align_bytes=256)
             nc.sync.dma_start(
                 out=raw[:].rearrange("p s j c -> p s (j c)"),
                 in_=rows.rearrange("(s p j) c -> p s (j c)", p=P, j=PACK),
@@ -196,11 +196,11 @@ def tile_moe_adp_gelu_kernel(
         activate(pre, spent)
         for b in range(BLOCKS):
             for e in range(E - LAG, E):
-                raw = stream.tile([P, PACK, P], F32, name="half", tag="stream", align_bytes=64)
+                raw = stream.tile([P, PACK, P], F32, name="half", tag="stream", align_bytes=256)
                 nc.sync.dma_start(out=raw[:], in_=wb[e, :, b * P : (b + 1) * P].rearrange("(p j) c -> p j c", j=PACK))
                 second_layer(e, b, raw[:], nc.vector.tensor_copy if e == E - 1 else nc.scalar.copy)
 
-        w_sb = stream.tile([P, PASSES, N], I32, name="w_sb", tag="stream", align_bytes=64)
+        w_sb = stream.tile([P, PASSES, N], I32, name="w_sb", tag="stream", align_bytes=256)
         nc.sync.dma_start(out=w_sb[:], in_=w_words.rearrange("s p n d -> p s (n d)").bitcast(I32))
 
         base_turned = bank(0, 0)
@@ -252,7 +252,7 @@ def tile_moe_adp_gelu_kernel(
                     start=(place == 0),
                     stop=(place == len(steps) - 1),
                 )
-            total_sb = keep.tile([P, T // 2], F32, name=label)
+            total_sb = keep.tile([P, T // 2], F32, name=label, align_bytes=256)
             nc.scalar.copy(out=total_sb[:], in_=total[:, : CHUNKS // 2, :].rearrange("p c t -> p (c t)"))
             return total_sb[:]
 
@@ -270,7 +270,7 @@ def tile_moe_adp_gelu_kernel(
         for tokens in halves:
             nc.vector.tensor_tensor(both[:, tokens], choices[0][:, tokens], choices[1][:, tokens], ADD)
         for tokens in halves:
-            second = twin.tile([P, T // 2], F32, name="second")
+            second = twin.tile([P, T // 2], F32, name="second", align_bytes=256)
             nc.vector.tensor_tensor(
                 second[:], both[:, tokens], base[:].rearrange("p c t -> p (c t)")[:, tokens], ADD
             )

@@ -24,9 +24,9 @@ PASSES = K // K_PASS
 BLOCKS = N // P
 CHUNKS = T // P
 PAIR = 2 * C
-STREAM_BUFS = 8
+RING_BYTES = 128 * 1024
 LAG = 2
-PER_BANK = (2, 4)
+BANK_GROUPS = (((0, 1, 2, 3), (4, 5, 6), (7,)), ((0, 1, 2, 3), (4, 5, 6, 7)))
 
 
 def tile_moe_adp_gelu_kernel(
@@ -35,7 +35,7 @@ def tile_moe_adp_gelu_kernel(
     nc = tc.nc
     with ExitStack() as ctx:
         keep = ctx.enter_context(tc.tile_pool(name="keep", bufs=1))
-        stream = ctx.enter_context(tc.tile_pool(name="stream", bufs=STREAM_BUFS))
+        stream = ctx.enter_context(tc.tile_pool(name="stream", bufs=1))
         twin = ctx.enter_context(tc.tile_pool(name="twin", bufs=2))
         work = ctx.enter_context(tc.tile_pool(name="work", bufs=8))
         coded = ctx.enter_context(tc.tile_pool(name="coded", bufs=16))
@@ -53,6 +53,7 @@ def tile_moe_adp_gelu_kernel(
         gate_sb = keep.tile([P, 2, T], F32, name="gate_sb")
         y_sb = [keep.tile([P, E * C], F32, name="y%d_sb" % b) for b in range(BLOCKS)]
 
+        idle = psum_y.tile([P, T], F32, name="idle", tag="idle")
         nc.gpsimd.memset(xs_sb[:], 0)
 
         def bank(b, turn):
@@ -81,43 +82,69 @@ def tile_moe_adp_gelu_kernel(
                 nc.vector.tensor_copy(words[:, s, :], x_sb[:, s, :].bitcast(U32).indirect(entries))
             return words, plane
 
+        ring = [0]
+
+        def ring_tile(shape, dtype):
+            size = 4
+            for extent in shape[1:]:
+                size = size * extent
+            start = ring[-1] if ring[-1] + size <= RING_BYTES else 0
+            ring.append(start + size)
+            return stream.tile(shape, dtype, name="ring%d" % len(ring), offset=start, align_bytes=256)
+
         def load_rows(rows):
             passes = rows.shape[0] // K_PASS
-            raw = stream.tile([P, passes, PACK, rows.shape[1]], F32, name="raw", tag="stream", align_bytes=256)
+            raw = ring_tile([P, passes, PACK, rows.shape[1]], F32)
             nc.sync.dma_start(
                 out=raw[:].rearrange("p s j c -> p s (j c)"),
                 in_=rows.rearrange("(s p j) c -> p s (j c)", p=P, j=PACK),
             )
             return raw
 
-        def quantize(values, pool, label):
+        def quantize(values, pool, label, tag=None):
             width = values.shape[1] // PACK
-            codes = pool.tile([P, width], U32, name=label + "_codes", align_bytes=64)
+            if tag is None:
+                codes = pool.tile([P, width], U32, name=label + "_codes", align_bytes=64)
+            else:
+                codes = keep.tile([P, width], U32, name=label + "_codes", tag=tag, align_bytes=64)
             plane = pool.tile([P, width], U8, name=label + "_plane", align_bytes=64)
             nc.vector.quantize_mx(out=codes[:].bitcast(FP8X4), scales=plane[:], in_=values)
             return codes, plane
 
-        def activate(pre, host):
-            h = host.rearrange("p j c -> p (j c)")[:, H // 2 : H].bitcast(BF16)
+        def warm_up(codes, plane):
+            for turn in range(2):
+                nc.tensor.matmul_mx(
+                    out=idle[:],
+                    lhsT=codes[:, :P].bitcast(FP8X4),
+                    lhsT_scale=plane[:, :P],
+                    rhs=x_sb[:, 0, :].bitcast(FP8X4),
+                    rhs_scale=xs_sb[:],
+                    start=True,
+                    stop=True,
+                )
+
+        def spent_bytes(host):
+            return host.rearrange("p j c -> p (j c)")[:, H // 2 : H].bitcast(BF16)
+
+        def activate(pre, h):
             nc.scalar.activation(
                 out=h.rearrange("p (c t) -> p c t", t=PACK), in_=pre[:].rearrange("p t c -> p c t"), func=GELU
             )
-            hidden.append(quantize(h, coded, "h"))
 
         def first_layer(e, earlier):
             words, plane = gathered[e // 2]
             cols = slice((e % 2) * C, (e % 2 + 1) * C)
             pre = psum.tile([P, PACK, C], F32, name="pre", tag="sums")
-            per_load = 2 if e < E - 2 else 1
             for s in range(PASSES):
-                if s % per_load == 0:
-                    loaded = load_rows(wa[e, s * K_PASS : (s + per_load) * K_PASS, :])
-                raw = loaded[:, s % per_load]
+                raw = load_rows(wa[e, s * K_PASS : (s + 1) * K_PASS, :])[:, 0]
                 source = raw.rearrange("p j (m u v) -> p u m j v", u=2, v=2)
                 for u, copy in enumerate((nc.vector.tensor_copy, nc.scalar.copy)):
                     grouped = work.tile([P, 2, P, PACK], BF16, name="a_grouped", align_bytes=64)
                     copy(out=grouped[:].rearrange("p v m j -> p m j v"), in_=source[:, u])
-                    a_codes, a_plane = quantize(grouped[:].rearrange("p v m j -> p (v m j)"), coded, "a")
+                    last = e == E - 1 and s == PASSES - 1 and u == 1
+                    a_codes, a_plane = quantize(
+                        grouped[:].rearrange("p v m j -> p (v m j)"), coded, "a", "last_codes" if last else None
+                    )
                     for v in range(2):
                         nc.tensor.matmul_mx(
                             out=pre[:, 2 * u + v, :],
@@ -128,44 +155,57 @@ def tile_moe_adp_gelu_kernel(
                             start=(s == 0 and u == 0 and v == 0),
                             stop=(s == PASSES - 1 and u == 1 and v == 1),
                         )
+                if e == E - 1 and s >= PASSES - 2:
+                    warm_up(a_codes, a_plane)
                 if e > 0 and s == 0:
-                    activate(earlier, raw)
+                    activate(earlier, spent_bytes(raw))
+                    hidden.append(quantize(spent_bytes(raw), keep, "h%d" % e))
             return pre
 
-        def second_layer(e, b, raw, copy):
-            h_codes, h_plane = hidden[e]
-            turn, place = divmod(e, PER_BANK[b])
-            grouped = work.tile([P, P, PACK], BF16, name="b_grouped", align_bytes=64)
+        def weave(raw, copy, held=None):
+            if held is None:
+                grouped = work.tile([P, P, PACK], BF16, name="b_grouped", align_bytes=64)
+            else:
+                grouped = keep.tile([P, P, PACK], BF16, name="b_grouped", tag=held, align_bytes=64)
             copy(
                 out=grouped[:].rearrange("p (c i) j -> p c j i", i=4),
                 in_=raw.rearrange("p j (c i) -> p c j i", i=4),
             )
-            b_codes, b_plane = quantize(grouped[:].rearrange("p c j -> p (c j)"), work, "b")
+            return grouped[:].rearrange("p c j -> p (c j)")
+
+        def second_layer(e, b, woven, held=None):
+            h_codes, h_plane = hidden[e]
+            turn, group = [(i, g) for i, g in enumerate(BANK_GROUPS[b]) if e in g][0]
+            place = group.index(e)
+            b_codes, b_plane = quantize(woven, work, "b", held)
             if place == 0:
                 y_ps[b] = bank(b, turn)
             nc.tensor.matmul_mx(
                 out=y_ps[b][:, place, :],
                 lhsT=b_codes[:].bitcast(FP8X4),
                 lhsT_scale=b_plane[:],
-                rhs=h_codes[:].bitcast(FP8X4),
-                rhs_scale=h_plane[:],
+                rhs=h_codes[:, :].bitcast(FP8X4),
+                rhs_scale=h_plane[:, :],
                 start=True,
                 stop=True,
             )
-            if place == PER_BANK[b] - 1:
+            if e == E - 1 and b == 0:
+                warm_up(b_codes, b_plane)
+            if place == len(group) - 1:
                 nc.scalar.copy(
-                    out=y_sb[b][:, turn * PER_BANK[b] * C : (e + 1) * C],
-                    in_=y_ps[b][:, : PER_BANK[b], :].rearrange("p a c -> p (a c)"),
+                    out=y_sb[b][:, group[0] * C : (e + 1) * C],
+                    in_=y_ps[b][:, : len(group), :].rearrange("p a c -> p (a c)"),
                 )
 
         def second_layer_whole(e):
             raw = load_rows(wb[e])[:, 0]
-            second_layer(e, 0, raw[:, :, :P], nc.vector.tensor_copy)
-            second_layer(e, 1, raw[:, :, P:], nc.scalar.copy)
-            return raw
+            second_layer(e, 0, weave(raw[:, :, :P], nc.vector.tensor_copy))
+            second_layer(e, 1, weave(raw[:, :, P:], nc.scalar.copy))
 
         def spread_gates():
-            nc.sync.dma_start(out=gate_rows[: 2 * CHUNKS, :], in_=gate[:, 0, :].rearrange("r (c m) -> r c m", m=P))
+            step = CHUNKS * T * 8 - T + P
+            flat = gate.rearrange("r p t -> (r p t)")[3 * T : 3 * T + 2 * CHUNKS * step]
+            nc.sync.dma_start(out=gate_rows[: 2 * CHUNKS, :], in_=flat.rearrange("(m s) -> m s", s=step)[:, :P])
             upright = psum_y.tile([P, P], F32, name="upright", tag="spread")
             nc.tensor.transpose(upright[:], gate_rows[:], ident[:])
             nc.scalar.copy(out=gate_columns[:], in_=upright[:, : 2 * CHUNKS])
@@ -188,27 +228,46 @@ def tile_moe_adp_gelu_kernel(
                 for q in range(4):
                     load_scale_rows(ws_sb, w_scales, q)
             if e == 1:
-                nc.sync.dma_start(pos_sb[0][:], pos1)
-                nc.sync.dma_start(pos_sb[1][:], pos2)
                 spread_gates()
             if e >= LAG:
-                spent = second_layer_whole(e - LAG)
-        activate(pre, spent)
+                second_layer_whole(e - LAG)
+        last_h = keep.tile([P, H], BF16, name="last_h", tag="last_h", align_bytes=64)
+        activate(pre, last_h[:])
+        whole = load_rows(wb[E - 2])[:, 0]
+        last = []
         for b in range(BLOCKS):
-            for e in range(E - LAG, E):
-                raw = stream.tile([P, PACK, P], F32, name="half", tag="stream", align_bytes=256)
-                nc.sync.dma_start(out=raw[:], in_=wb[e, :, b * P : (b + 1) * P].rearrange("(p j) c -> p j c", j=PACK))
-                second_layer(e, b, raw[:], nc.vector.tensor_copy if e == E - 1 else nc.scalar.copy)
+            raw = ring_tile([P, PACK, P], F32)
+            nc.sync.dma_start(out=raw[:], in_=wb[E - 1, :, b * P : (b + 1) * P].rearrange("(p j) c -> p j c", j=PACK))
+            last.append(raw)
+            if b == 0:
+                spent = ring[-1] - PACK * P * 4
+        second_layer(E - 2, 0, weave(whole[:, :, :P], nc.vector.tensor_copy))
+        woven = weave(last[0][:], nc.vector.tensor_copy, "last_woven")
+        h_codes = stream.tile([P, C], U32, name="last_h_codes", offset=spent, align_bytes=256)
+        h_plane = keep.tile([P, C], U8, name="last_h_plane", align_bytes=64)
+        nc.vector.quantize_mx(out=h_codes[:].bitcast(FP8X4), scales=h_plane[:], in_=last_h[:])
+        hidden.append((h_codes, h_plane))
+        second_layer(E - 1, 0, woven)
+        second_layer(E - 2, 1, weave(whole[:, :, P:], nc.scalar.copy, "last_codes"), "last_woven")
+        second_layer(E - 1, 1, weave(last[1][:], nc.vector.tensor_copy, "last_h"))
+        nc.sync.dma_start(pos_sb[0][:], pos1)
+        nc.sync.dma_start(pos_sb[1][:], pos2)
 
-        w_sb = stream.tile([P, PASSES, N], I32, name="w_sb", tag="stream", align_bytes=256)
+        w_sb = ring_tile([P, PASSES, N], I32)
         nc.sync.dma_start(out=w_sb[:], in_=w_words.rearrange("s p n d -> p s (n d)").bitcast(I32))
 
-        base_turned = bank(0, 0)
+        def half_bank(half, shape):
+            return psum_y.tile(shape, F32, name="half_bank", tag=("bank0_0", "spread")[half])
+
+        base_sb = keep.tile([P, T], F32, name="base_sb")
         for c in range(CHUNKS):
+            half, place = divmod(c, CHUNKS // 2)
+            if place == 0:
+                base_turned = half_bank(half, [P, CHUNKS // 2, P])
             tokens = slice(c * P, (c + 1) * P)
             for s in range(PASSES):
                 nc.tensor.matmul_mx(
-                    out=base_turned[:, c, :],
+                    out=base_turned[:, place, :],
                     lhsT=x_sb[:, s, tokens].bitcast(FP8X4),
                     lhsT_scale=xs_sb[4 * s : P, tokens],
                     rhs=w_sb[:, s, :P].bitcast(FP8X4),
@@ -216,20 +275,11 @@ def tile_moe_adp_gelu_kernel(
                     start=(s == 0),
                     stop=(s == PASSES - 1),
                 )
-        base_sb = keep.tile([P, T], F32, name="base_sb")
-        nc.scalar.copy(out=base_sb[:], in_=base_turned[:].rearrange("p c n -> p (c n)"))
-
-        base = bank(1, 0)
-        for s in range(PASSES):
-            nc.tensor.matmul_mx(
-                out=base[:].rearrange("p c t -> p (c t)"),
-                lhsT=w_sb[:, s, P:].bitcast(FP8X4),
-                lhsT_scale=ws_sb[4 * s : P, P:],
-                rhs=x_sb[:, s, :].bitcast(FP8X4),
-                rhs_scale=xs_sb[4 * s : P, :],
-                start=(s == 0),
-                stop=(s == PASSES - 1),
-            )
+            if place == CHUNKS // 2 - 1:
+                nc.scalar.copy(
+                    out=base_sb[:, half * T // 2 : (half + 1) * T // 2],
+                    in_=base_turned[:].rearrange("p c n -> p (c n)"),
+                )
 
         halves = [slice(half * T // 2, (half + 1) * T // 2) for half in range(2)]
 
@@ -256,22 +306,38 @@ def tile_moe_adp_gelu_kernel(
             nc.scalar.copy(out=total_sb[:], in_=total[:, : CHUNKS // 2, :].rearrange("p c t -> p (c t)"))
             return total_sb[:]
 
+        def frozen_half(half):
+            total = psum_y.tile([P, T // 2], F32, name="frozen", tag=("bank1_0", "bank0_1")[half])
+            for s in range(PASSES):
+                nc.tensor.matmul_mx(
+                    out=total[:],
+                    lhsT=w_sb[:, s, P:].bitcast(FP8X4),
+                    lhsT_scale=ws_sb[4 * s : P, P:],
+                    rhs=x_sb[:, s, halves[half]].bitcast(FP8X4),
+                    rhs_scale=xs_sb[4 * s : P, halves[half]],
+                    start=(s == 0),
+                    stop=(s == PASSES - 1),
+                )
+            return total
+
         choice = gated_choice(0, 0)
         routed = []
         for half, tokens in enumerate(halves):
-            total = psum.tile([P, CHUNKS, P], F32, name="routed", tag="sums")
+            total = half_bank(half, [P, CHUNKS, P])
             routed.append(add_turned((choice[:, tokens], gated_choice(0, 1, half)), total, "routed%d" % half))
+        base = [frozen_half(0)]
         for half, tokens in enumerate(halves):
-            result = add_turned((base_sb[:, tokens], routed[half]), bank(half, 1), "result%d" % half)
+            total = psum.tile([P, CHUNKS, P], F32, name="total", tag="sums")
+            result = add_turned((base_sb[:, tokens], routed[half]), total, "result%d" % half)
             nc.scalar.dma_start(out=out[:P, tokens], in_=result)
 
-        choices = [gated_choice(1, r) for r in range(2)]
+        base.append(frozen_half(1))
+        choice = gated_choice(1, 0)
+        others = [gated_choice(1, 1, half) for half in range(2)]
         both = keep.tile([P, T], F32, name="both")
-        for tokens in halves:
-            nc.vector.tensor_tensor(both[:, tokens], choices[0][:, tokens], choices[1][:, tokens], ADD)
-        for tokens in halves:
+        for half, tokens in enumerate(halves):
+            nc.vector.tensor_tensor(both[:, tokens], choice[:, tokens], others[half], ADD)
+        for half, tokens in enumerate(halves):
             second = twin.tile([P, T // 2], F32, name="second", align_bytes=256)
-            nc.vector.tensor_tensor(
-                second[:], both[:, tokens], base[:].rearrange("p c t -> p (c t)")[:, tokens], ADD
-            )
+            nc.vector.tensor_tensor(second[:], both[:, tokens], base[half][:], ADD)
             nc.sync.dma_start(out=out[P:, tokens], in_=second[:])

@@ -16,6 +16,7 @@ FP8X4 = mybir.dt.float8_e4m3fn_x4
 MULT = mybir.AluOpType.mult
 ADD = mybir.AluOpType.add
 GELU = mybir.ActivationFunctionType.Gelu_apprx_tanh
+COPY = mybir.ActivationFunctionType.Copy
 
 P = 128
 PACK = 4
@@ -26,7 +27,7 @@ CHUNKS = T // P
 PAIR = 2 * C
 RING_BYTES = 128 * 1024
 LAG = 2
-BANK_GROUPS = (((0, 1, 2, 3), (4, 5, 6), (7,)), ((0, 1, 2, 3), (4, 5, 6, 7)))
+BANK_GROUPS = (((0, 1, 2, 3), (4, 5, 6), (7,)), ((0, 1, 2, 3), (4, 5, 6), (7,)))
 
 
 def tile_moe_adp_gelu_kernel(
@@ -192,7 +193,8 @@ def tile_moe_adp_gelu_kernel(
             if e == E - 1 and b == 0:
                 warm_up(b_codes, b_plane)
             if place == len(group) - 1:
-                nc.scalar.copy(
+                copy = nc.vector.tensor_copy if (e, b) == (E - 1, 1) else nc.scalar.copy
+                copy(
                     out=y_sb[b][:, group[0] * C : (e + 1) * C],
                     in_=y_ps[b][:, : len(group), :].rearrange("p a c -> p (a c)"),
                 )
@@ -256,43 +258,54 @@ def tile_moe_adp_gelu_kernel(
         w_sb = ring_tile([P, PASSES, N], I32)
         nc.sync.dma_start(out=w_sb[:], in_=w_words.rearrange("s p n d -> p s (n d)").bitcast(I32))
 
-        def half_bank(half, shape):
-            return psum_y.tile(shape, F32, name="half_bank", tag=("bank0_0", "spread")[half])
+        halves = [slice(half * T // 2, (half + 1) * T // 2) for half in range(2)]
+        half_chunks = CHUNKS // 2
 
-        base_sb = keep.tile([P, T], F32, name="base_sb")
-        for c in range(CHUNKS):
-            half, place = divmod(c, CHUNKS // 2)
-            if place == 0:
-                base_turned = half_bank(half, [P, CHUNKS // 2, P])
-            tokens = slice(c * P, (c + 1) * P)
+        def entries(r, tokens):
+            return pos_sb[r][:, tokens.start // 16 : tokens.stop // 16]
+
+        def gated_choice(b, r, tokens):
+            gated = keep.tile([P, tokens.stop - tokens.start], F32, name="gated%d_%d_%d" % (b, r, tokens.start))
+            nc.vector.tensor_tensor(gated[:], y_sb[b][:].indirect(entries(r, tokens)), gate_sb[:, r, tokens], MULT)
+            return gated[:]
+
+        def plain_choice(r):
+            picked = keep.tile([P, T // 2], F32, name="picked%d" % r)
+            nc.scalar.activation(out=picked[:], in_=y_sb[0][:].indirect(entries(r, halves[0])), func=COPY)
+            return picked[:]
+
+        def frozen_turned(half, tag):
+            shared = psum_y.tile([P, CHUNKS, P], F32, name="shared", tag=tag)
+            for c in range(half_chunks):
+                tokens = slice((half * half_chunks + c) * P, (half * half_chunks + c + 1) * P)
+                for s in range(PASSES):
+                    nc.tensor.matmul_mx(
+                        out=shared[:, c, :],
+                        lhsT=x_sb[:, s, tokens].bitcast(FP8X4),
+                        lhsT_scale=xs_sb[4 * s : P, tokens],
+                        rhs=w_sb[:, s, :P].bitcast(FP8X4),
+                        rhs_scale=ws_sb[4 * s : P, :P],
+                        start=(s == 0),
+                        stop=(s == PASSES - 1),
+                    )
+            return shared
+
+        def frozen_upright(half, tag):
+            shared = psum_y.tile([P, CHUNKS, P], F32, name="shared", tag=tag)
             for s in range(PASSES):
                 nc.tensor.matmul_mx(
-                    out=base_turned[:, place, :],
-                    lhsT=x_sb[:, s, tokens].bitcast(FP8X4),
-                    lhsT_scale=xs_sb[4 * s : P, tokens],
-                    rhs=w_sb[:, s, :P].bitcast(FP8X4),
-                    rhs_scale=ws_sb[4 * s : P, :P],
+                    out=shared[:, :half_chunks, :].rearrange("p c t -> p (c t)"),
+                    lhsT=w_sb[:, s, P:].bitcast(FP8X4),
+                    lhsT_scale=ws_sb[4 * s : P, P:],
+                    rhs=x_sb[:, s, halves[half]].bitcast(FP8X4),
+                    rhs_scale=xs_sb[4 * s : P, halves[half]],
                     start=(s == 0),
                     stop=(s == PASSES - 1),
                 )
-            if place == CHUNKS // 2 - 1:
-                nc.scalar.copy(
-                    out=base_sb[:, half * T // 2 : (half + 1) * T // 2],
-                    in_=base_turned[:].rearrange("p c n -> p (c n)"),
-                )
+            return shared
 
-        halves = [slice(half * T // 2, (half + 1) * T // 2) for half in range(2)]
-
-        def gated_choice(b, r, half=None):
-            tokens = slice(0, T) if half is None else halves[half]
-            width = tokens.stop - tokens.start
-            picked = keep.tile([P, width], F32, name="gated%d_%d_%d" % (b, r, tokens.start))
-            entries = pos_sb[r][:, tokens.start // 16 : tokens.stop // 16]
-            nc.vector.tensor_tensor(picked[:], y_sb[b][:].indirect(entries), gate_sb[:, r, tokens], MULT)
-            return picked[:]
-
-        def add_turned(terms, total, label):
-            steps = [(term, c) for term in terms for c in range(CHUNKS // 2)]
+        def add_turned(terms, total):
+            steps = [(term, c) for term in terms for c in range(half_chunks)]
             for place, (term, c) in enumerate(steps):
                 nc.tensor.matmul(
                     out=total[:, c, :],
@@ -302,42 +315,46 @@ def tile_moe_adp_gelu_kernel(
                     start=(place == 0),
                     stop=(place == len(steps) - 1),
                 )
-            total_sb = keep.tile([P, T // 2], F32, name=label, align_bytes=256)
-            nc.scalar.copy(out=total_sb[:], in_=total[:, : CHUNKS // 2, :].rearrange("p c t -> p (c t)"))
-            return total_sb[:]
 
-        def frozen_half(half):
-            total = psum_y.tile([P, T // 2], F32, name="frozen", tag=("bank1_0", "bank0_1")[half])
-            for s in range(PASSES):
-                nc.tensor.matmul_mx(
-                    out=total[:],
-                    lhsT=w_sb[:, s, P:].bitcast(FP8X4),
-                    lhsT_scale=ws_sb[4 * s : P, P:],
-                    rhs=x_sb[:, s, halves[half]].bitcast(FP8X4),
-                    rhs_scale=xs_sb[4 * s : P, halves[half]],
-                    start=(s == 0),
-                    stop=(s == PASSES - 1),
+        def finish_lower(half, terms):
+            total = psum.tile([P, half_chunks, P], F32, name="total", tag="sums")
+            add_turned(terms, total)
+            result = keep.tile([P, T // 2], F32, name="result%d" % half, align_bytes=256)
+            nc.scalar.copy(out=result[:], in_=total[:].rearrange("p c t -> p (c t)"))
+            nc.scalar.dma_start(out=out[:P, halves[half]], in_=result[:])
+
+        plain = [plain_choice(r) for r in range(2)]
+        gated = [gated_choice(0, r, halves[1]) for r in range(2)]
+        second_bank = frozen_turned(1, "bank0_0")
+        first_bank = frozen_turned(0, "spread")
+        add_turned(gated, second_bank[:, half_chunks:, :])
+        add_turned(plain[:1], first_bank[:, half_chunks:, :])
+        upper = [frozen_upright(0, "bank1_1")]
+        add_turned(plain[1:], upper[0][:, half_chunks:, :])
+
+        second_sb = keep.tile([P, T], F32, name="second_sb")
+        nc.scalar.copy(out=second_sb[:], in_=second_bank[:].rearrange("p c t -> p (c t)"))
+        first_sb = keep.tile([P, 3, T // 2], F32, name="first_sb")
+        nc.scalar.copy(out=first_sb[:, 0, :], in_=first_bank[:, :half_chunks, :].rearrange("p c t -> p (c t)"))
+        for r, shared in enumerate((first_bank, upper[0])):
+            for c in range(half_chunks):
+                nc.scalar.activation(
+                    out=first_sb[:, 1 + r, c * P : (c + 1) * P],
+                    in_=shared[:, half_chunks + c, :],
+                    func=COPY,
+                    scale=gate_columns[:, r * CHUNKS + c : r * CHUNKS + c + 1],
                 )
-            return total
+        finish_lower(1, [second_sb[:, tokens] for tokens in halves])
+        upper.append(frozen_upright(1, "bank0_1"))
+        finish_lower(0, [first_sb[:, term, :] for term in range(3)])
 
-        choice = gated_choice(0, 0)
-        routed = []
-        for half, tokens in enumerate(halves):
-            total = half_bank(half, [P, CHUNKS, P])
-            routed.append(add_turned((choice[:, tokens], gated_choice(0, 1, half)), total, "routed%d" % half))
-        base = [frozen_half(0)]
-        for half, tokens in enumerate(halves):
-            total = psum.tile([P, CHUNKS, P], F32, name="total", tag="sums")
-            result = add_turned((base_sb[:, tokens], routed[half]), total, "result%d" % half)
-            nc.scalar.dma_start(out=out[:P, tokens], in_=result)
-
-        base.append(frozen_half(1))
-        choice = gated_choice(1, 0)
-        others = [gated_choice(1, 1, half) for half in range(2)]
+        choice = gated_choice(1, 0, slice(0, T))
+        others = [gated_choice(1, 1, tokens) for tokens in halves]
         both = keep.tile([P, T], F32, name="both")
         for half, tokens in enumerate(halves):
             nc.vector.tensor_tensor(both[:, tokens], choice[:, tokens], others[half], ADD)
         for half, tokens in enumerate(halves):
             second = twin.tile([P, T // 2], F32, name="second", align_bytes=256)
-            nc.vector.tensor_tensor(second[:], both[:, tokens], base[half][:], ADD)
+            base = upper[half][:, :half_chunks, :].rearrange("p c t -> p (c t)")
+            nc.vector.tensor_tensor(second[:], both[:, tokens], base, ADD)
             nc.sync.dma_start(out=out[P:, tokens], in_=second[:])

@@ -27,7 +27,7 @@ CHUNKS = T // P
 PAIR = 2 * C
 RING_BYTES = 128 * 1024
 LAG = 2
-BANK_GROUPS = (((0, 1, 2, 3), (4, 5, 6), (7,)), ((0, 1, 2, 3), (4, 5, 6), (7,)))
+BANK_GROUPS = (((0, 1, 2, 3), (4, 5, 6), (7,)), ((0, 1, 2, 3), (4, 5), (6,), (7,)))
 
 
 def tile_moe_adp_gelu_kernel(
@@ -39,7 +39,7 @@ def tile_moe_adp_gelu_kernel(
         stream = ctx.enter_context(tc.tile_pool(name="stream", bufs=1))
         twin = ctx.enter_context(tc.tile_pool(name="twin", bufs=2))
         work = ctx.enter_context(tc.tile_pool(name="work", bufs=8))
-        coded = ctx.enter_context(tc.tile_pool(name="coded", bufs=16))
+        coded = ctx.enter_context(tc.tile_pool(name="coded", bufs=12))
         psum = ctx.enter_context(tc.psum_pool(name="psum", bufs=2))
         psum_y = ctx.enter_context(tc.psum_pool(name="psum_y", bufs=1))
 
@@ -55,6 +55,8 @@ def tile_moe_adp_gelu_kernel(
         y_sb = [keep.tile([P, E * C], F32, name="y%d_sb" % b) for b in range(BLOCKS)]
 
         idle = psum_y.tile([P, T], F32, name="idle", tag="idle")
+        wide_codes = keep.tile([P, H], U32, name="wide_codes", align_bytes=64)
+        wide_plane = keep.tile([P, H], U8, name="wide_plane", align_bytes=64)
         nc.gpsimd.memset(xs_sb[:], 0)
 
         def bank(b, turn):
@@ -75,7 +77,10 @@ def tile_moe_adp_gelu_kernel(
         nc.gpsimd.memset(ws_sb[:], 0)
 
         def gather_pair(g):
-            words = twin.tile([P, PASSES, PAIR], U32, name="slot_words", align_bytes=64)
+            if g < E // 2 - 1:
+                words = twin.tile([P, PASSES, PAIR], U32, name="slot_words", align_bytes=64)
+            else:
+                words = keep.tile([P, PASSES, PAIR], U32, name="last_words", tag="last_words", align_bytes=64)
             plane = twin.tile([P, PAIR], U8, name="slot_plane", align_bytes=64)
             entries = offs_sb[:, g * PAIR // 16 : (g + 1) * PAIR // 16]
             nc.vector.tensor_copy(plane[:], xs_sb[:].indirect(entries))
@@ -112,14 +117,14 @@ def tile_moe_adp_gelu_kernel(
             nc.vector.quantize_mx(out=codes[:].bitcast(FP8X4), scales=plane[:], in_=values)
             return codes, plane
 
-        def warm_up(codes, plane):
-            for turn in range(2):
+        def warm_up(codes, plane, passes):
+            for turn in range(passes):
                 nc.tensor.matmul_mx(
                     out=idle[:],
                     lhsT=codes[:, :P].bitcast(FP8X4),
                     lhsT_scale=plane[:, :P],
-                    rhs=x_sb[:, 0, :].bitcast(FP8X4),
-                    rhs_scale=xs_sb[:],
+                    rhs=wide_codes[:].bitcast(FP8X4),
+                    rhs_scale=wide_plane[:],
                     start=True,
                     stop=True,
                 )
@@ -136,28 +141,42 @@ def tile_moe_adp_gelu_kernel(
             words, plane = gathered[e // 2]
             cols = slice((e % 2) * C, (e % 2 + 1) * C)
             pre = psum.tile([P, PACK, C], F32, name="pre", tag="sums")
+            waiting = []
+            done = []
+
+            def multiply(s, u, a_codes, a_plane):
+                for v in range(2):
+                    done.append((s, u, v))
+                    nc.tensor.matmul_mx(
+                        out=pre[:, 2 * u + v, :],
+                        lhsT=a_codes[:, v * P : (v + 1) * P].bitcast(FP8X4),
+                        lhsT_scale=a_plane[:, v * P : (v + 1) * P],
+                        rhs=words[:, s, cols].bitcast(FP8X4),
+                        rhs_scale=plane[4 * s : P, cols],
+                        start=(len(done) == 1),
+                        stop=(len(done) == PASSES * PACK),
+                    )
+
             for s in range(PASSES):
                 raw = load_rows(wa[e, s * K_PASS : (s + 1) * K_PASS, :])[:, 0]
                 source = raw.rearrange("p j (m u v) -> p u m j v", u=2, v=2)
                 for u, copy in enumerate((nc.vector.tensor_copy, nc.scalar.copy)):
                     grouped = work.tile([P, 2, P, PACK], BF16, name="a_grouped", align_bytes=64)
                     copy(out=grouped[:].rearrange("p v m j -> p m j v"), in_=source[:, u])
-                    last = e == E - 1 and s == PASSES - 1 and u == 1
-                    a_codes, a_plane = quantize(
-                        grouped[:].rearrange("p v m j -> p (v m j)"), coded, "a", "last_codes" if last else None
-                    )
-                    for v in range(2):
-                        nc.tensor.matmul_mx(
-                            out=pre[:, 2 * u + v, :],
-                            lhsT=a_codes[:, v * P : (v + 1) * P].bitcast(FP8X4),
-                            lhsT_scale=a_plane[:, v * P : (v + 1) * P],
-                            rhs=words[:, s, cols].bitcast(FP8X4),
-                            rhs_scale=plane[4 * s : P, cols],
-                            start=(s == 0 and u == 0 and v == 0),
-                            stop=(s == PASSES - 1 and u == 1 and v == 1),
-                        )
-                if e == E - 1 and s >= PASSES - 2:
-                    warm_up(a_codes, a_plane)
+                    values = grouped[:].rearrange("p v m j -> p (v m j)")
+                    if e == E - 1 and s == PASSES - 2:
+                        a_codes = wide_codes[:, u * 2 * P : (u + 1) * 2 * P]
+                        a_plane = wide_plane[:, u * 2 * P : (u + 1) * 2 * P]
+                        nc.vector.quantize_mx(out=a_codes.bitcast(FP8X4), scales=a_plane, in_=values)
+                    else:
+                        a_codes, a_plane = quantize(values, coded, "a")
+                    waiting.append((s, u, a_codes, a_plane))
+                    if e < E - 1 or s >= PASSES - 2:
+                        for step in waiting[-1:] + waiting[:-1]:
+                            multiply(*step)
+                        waiting.clear()
+                if e == E - 1 and s == PASSES - 1:
+                    warm_up(a_codes, a_plane, 2)
                 if e > 0 and s == 0:
                     activate(earlier, spent_bytes(raw))
                     hidden.append(quantize(spent_bytes(raw), keep, "h%d" % e))
@@ -190,8 +209,8 @@ def tile_moe_adp_gelu_kernel(
                 start=True,
                 stop=True,
             )
-            if e == E - 1 and b == 0:
-                warm_up(b_codes, b_plane)
+            if (e, b) == (E - 1, 0):
+                warm_up(b_codes, b_plane, 2)
             if place == len(group) - 1:
                 copy = nc.vector.tensor_copy if (e, b) == (E - 1, 1) else nc.scalar.copy
                 copy(
@@ -250,13 +269,18 @@ def tile_moe_adp_gelu_kernel(
         nc.vector.quantize_mx(out=h_codes[:].bitcast(FP8X4), scales=h_plane[:], in_=last_h[:])
         hidden.append((h_codes, h_plane))
         second_layer(E - 1, 0, woven)
-        second_layer(E - 2, 1, weave(whole[:, :, P:], nc.scalar.copy, "last_codes"), "last_woven")
+        second_layer(E - 2, 1, weave(whole[:, :, P:], nc.scalar.copy, "last_words"), "last_woven")
         second_layer(E - 1, 1, weave(last[1][:], nc.vector.tensor_copy, "last_h"))
+
+        def load_frozen(b):
+            words = ring_tile([P, PASSES, P], I32)
+            source = w_words.rearrange("s p n d -> p s (n d)").bitcast(I32)
+            nc.sync.dma_start(out=words[:], in_=source[:, :, b * P : (b + 1) * P])
+            return words
+
         nc.sync.dma_start(pos_sb[0][:], pos1)
         nc.sync.dma_start(pos_sb[1][:], pos2)
-
-        w_sb = ring_tile([P, PASSES, N], I32)
-        nc.sync.dma_start(out=w_sb[:], in_=w_words.rearrange("s p n d -> p s (n d)").bitcast(I32))
+        w_sb = [load_frozen(b) for b in range(BLOCKS)]
 
         halves = [slice(half * T // 2, (half + 1) * T // 2) for half in range(2)]
         half_chunks = CHUNKS // 2
@@ -274,16 +298,16 @@ def tile_moe_adp_gelu_kernel(
             nc.scalar.activation(out=picked[:], in_=y_sb[0][:].indirect(entries(r, halves[0])), func=COPY)
             return picked[:]
 
-        def frozen_turned(half, tag):
+        def frozen_turned(chunks, tag):
             shared = psum_y.tile([P, CHUNKS, P], F32, name="shared", tag=tag)
-            for c in range(half_chunks):
-                tokens = slice((half * half_chunks + c) * P, (half * half_chunks + c + 1) * P)
+            for place, c in enumerate(chunks):
+                tokens = slice(c * P, (c + 1) * P)
                 for s in range(PASSES):
                     nc.tensor.matmul_mx(
-                        out=shared[:, c, :],
+                        out=shared[:, place, :],
                         lhsT=x_sb[:, s, tokens].bitcast(FP8X4),
                         lhsT_scale=xs_sb[4 * s : P, tokens],
-                        rhs=w_sb[:, s, :P].bitcast(FP8X4),
+                        rhs=w_sb[0][:, s, :].bitcast(FP8X4),
                         rhs_scale=ws_sb[4 * s : P, :P],
                         start=(s == 0),
                         stop=(s == PASSES - 1),
@@ -295,7 +319,7 @@ def tile_moe_adp_gelu_kernel(
             for s in range(PASSES):
                 nc.tensor.matmul_mx(
                     out=shared[:, :half_chunks, :].rearrange("p c t -> p (c t)"),
-                    lhsT=w_sb[:, s, P:].bitcast(FP8X4),
+                    lhsT=w_sb[1][:, s, :].bitcast(FP8X4),
                     lhsT_scale=ws_sb[4 * s : P, P:],
                     rhs=x_sb[:, s, halves[half]].bitcast(FP8X4),
                     rhs_scale=xs_sb[4 * s : P, halves[half]],
@@ -305,7 +329,7 @@ def tile_moe_adp_gelu_kernel(
             return shared
 
         def add_turned(terms, total):
-            steps = [(term, c) for term in terms for c in range(half_chunks)]
+            steps = [(term, c) for c in range(half_chunks) for term in terms]
             for place, (term, c) in enumerate(steps):
                 nc.tensor.matmul(
                     out=total[:, c, :],
@@ -325,28 +349,30 @@ def tile_moe_adp_gelu_kernel(
 
         plain = [plain_choice(r) for r in range(2)]
         gated = [gated_choice(0, r, halves[1]) for r in range(2)]
-        second_bank = frozen_turned(1, "bank0_0")
-        first_bank = frozen_turned(0, "spread")
+        first_banks = [frozen_turned([c], tag) for c, tag in enumerate(("spread", "bank0_1"))]
+        second_bank = frozen_turned([2, 3], "bank0_0")
         add_turned(gated, second_bank[:, half_chunks:, :])
-        add_turned(plain[:1], first_bank[:, half_chunks:, :])
-        upper = [frozen_upright(0, "bank1_1")]
-        add_turned(plain[1:], upper[0][:, half_chunks:, :])
+        for r in range(2):
+            for c in range(half_chunks):
+                nc.tensor.transpose(first_banks[c][:, 1 + r, :], plain[r][:, c * P : (c + 1) * P], ident[:])
+        upper = [frozen_upright(0, "bank1_0")]
 
         second_sb = keep.tile([P, T], F32, name="second_sb")
         nc.scalar.copy(out=second_sb[:], in_=second_bank[:].rearrange("p c t -> p (c t)"))
         first_sb = keep.tile([P, 3, T // 2], F32, name="first_sb")
-        nc.scalar.copy(out=first_sb[:, 0, :], in_=first_bank[:, :half_chunks, :].rearrange("p c t -> p (c t)"))
-        for r, shared in enumerate((first_bank, upper[0])):
-            for c in range(half_chunks):
+        for c in range(half_chunks):
+            columns = slice(c * P, (c + 1) * P)
+            nc.scalar.copy(out=first_sb[:, 0, columns], in_=first_banks[c][:, 0, :])
+            for r in range(2):
                 nc.scalar.activation(
-                    out=first_sb[:, 1 + r, c * P : (c + 1) * P],
-                    in_=shared[:, half_chunks + c, :],
+                    out=first_sb[:, 1 + r, columns],
+                    in_=first_banks[c][:, 1 + r, :],
                     func=COPY,
                     scale=gate_columns[:, r * CHUNKS + c : r * CHUNKS + c + 1],
                 )
         finish_lower(1, [second_sb[:, tokens] for tokens in halves])
-        upper.append(frozen_upright(1, "bank0_1"))
         finish_lower(0, [first_sb[:, term, :] for term in range(3)])
+        upper.append(frozen_upright(1, "bank0_1"))
 
         choice = gated_choice(1, 0, slice(0, T))
         others = [gated_choice(1, 1, tokens) for tokens in halves]

@@ -26,8 +26,8 @@ BLOCKS = N // P
 CHUNKS = T // P
 PAIR = 2 * C
 RING_BYTES = 128 * 1024
-LAG = 2
-BANK_GROUPS = (((0, 1, 2, 3), (4, 5, 6), (7,)), ((0, 1, 2, 3), (4, 5), (6,), (7,)))
+LAG = 3
+BANK_GROUPS = (((0, 1, 2, 3), (4, 5, 6), (7,)), ((0, 1, 2, 3), (4, 5), (6, 7)))
 
 
 def tile_moe_adp_gelu_kernel(
@@ -77,10 +77,7 @@ def tile_moe_adp_gelu_kernel(
         nc.gpsimd.memset(ws_sb[:], 0)
 
         def gather_pair(g):
-            if g < E // 2 - 1:
-                words = twin.tile([P, PASSES, PAIR], U32, name="slot_words", align_bytes=64)
-            else:
-                words = keep.tile([P, PASSES, PAIR], U32, name="last_words", tag="last_words", align_bytes=64)
+            words = twin.tile([P, PASSES, PAIR], U32, name="slot_words", align_bytes=64)
             plane = twin.tile([P, PAIR], U8, name="slot_plane", align_bytes=64)
             entries = offs_sb[:, g * PAIR // 16 : (g + 1) * PAIR // 16]
             nc.vector.tensor_copy(plane[:], xs_sb[:].indirect(entries))
@@ -141,7 +138,6 @@ def tile_moe_adp_gelu_kernel(
             words, plane = gathered[e // 2]
             cols = slice((e % 2) * C, (e % 2 + 1) * C)
             pre = psum.tile([P, PACK, C], F32, name="pre", tag="sums")
-            waiting = []
             done = []
 
             def multiply(s, u, a_codes, a_plane):
@@ -169,14 +165,11 @@ def tile_moe_adp_gelu_kernel(
                         a_plane = wide_plane[:, u * 2 * P : (u + 1) * 2 * P]
                         nc.vector.quantize_mx(out=a_codes.bitcast(FP8X4), scales=a_plane, in_=values)
                     else:
-                        a_codes, a_plane = quantize(values, coded, "a")
-                    waiting.append((s, u, a_codes, a_plane))
-                    if e < E - 1 or s >= PASSES - 2:
-                        for step in waiting[-1:] + waiting[:-1]:
-                            multiply(*step)
-                        waiting.clear()
-                if e == E - 1 and s == PASSES - 1:
-                    warm_up(a_codes, a_plane, 2)
+                        last = e == E - 1 and s == PASSES - 1 and u == 1
+                        a_codes, a_plane = quantize(values, coded, "a", "last_codes" if last else None)
+                    multiply(s, u, a_codes, a_plane)
+                if e == E - 1 and s >= PASSES - 2:
+                    warm_up(a_codes, a_plane, (0, 0)[s - PASSES + 2])
                 if e > 0 and s == 0:
                     activate(earlier, spent_bytes(raw))
                     hidden.append(quantize(spent_bytes(raw), keep, "h%d" % e))
@@ -185,6 +178,8 @@ def tile_moe_adp_gelu_kernel(
         def weave(raw, copy, held=None):
             if held is None:
                 grouped = work.tile([P, P, PACK], BF16, name="b_grouped", align_bytes=64)
+            elif isinstance(held, int):
+                grouped = stream.tile([P, P, PACK], BF16, name="last_woven", offset=held, align_bytes=256)
             else:
                 grouped = keep.tile([P, P, PACK], BF16, name="b_grouped", tag=held, align_bytes=64)
             copy(
@@ -209,11 +204,9 @@ def tile_moe_adp_gelu_kernel(
                 start=True,
                 stop=True,
             )
-            if (e, b) == (E - 1, 0):
-                warm_up(b_codes, b_plane, 2)
+            warm_up(b_codes, b_plane, {(E - 3, 1): 1, (E - 2, 0): 1, (E - 1, 0): 2}.get((e, b), 0))
             if place == len(group) - 1:
-                copy = nc.vector.tensor_copy if (e, b) == (E - 1, 1) else nc.scalar.copy
-                copy(
+                nc.scalar.copy(
                     out=y_sb[b][:, group[0] * C : (e + 1) * C],
                     in_=y_ps[b][:, : len(group), :].rearrange("p a c -> p (a c)"),
                 )
@@ -252,7 +245,9 @@ def tile_moe_adp_gelu_kernel(
                 spread_gates()
             if e >= LAG:
                 second_layer_whole(e - LAG)
-        last_h = keep.tile([P, H], BF16, name="last_h", tag="last_h", align_bytes=64)
+        second_layer_whole(E - 3)
+        h_bytes = ring[-1] - PACK * N * 4
+        last_h = stream.tile([P, H], BF16, name="last_h", offset=h_bytes, align_bytes=256)
         activate(pre, last_h[:])
         whole = load_rows(wb[E - 2])[:, 0]
         last = []
@@ -269,8 +264,8 @@ def tile_moe_adp_gelu_kernel(
         nc.vector.quantize_mx(out=h_codes[:].bitcast(FP8X4), scales=h_plane[:], in_=last_h[:])
         hidden.append((h_codes, h_plane))
         second_layer(E - 1, 0, woven)
-        second_layer(E - 2, 1, weave(whole[:, :, P:], nc.scalar.copy, "last_words"), "last_woven")
-        second_layer(E - 1, 1, weave(last[1][:], nc.vector.tensor_copy, "last_h"))
+        second_layer(E - 2, 1, weave(whole[:, :, P:], nc.scalar.copy, "last_codes"), "last_woven")
+        second_layer(E - 1, 1, weave(last[1][:], nc.vector.tensor_copy, h_bytes))
 
         def load_frozen(b):
             words = ring_tile([P, PASSES, P], I32)
@@ -347,32 +342,32 @@ def tile_moe_adp_gelu_kernel(
             nc.scalar.copy(out=result[:], in_=total[:].rearrange("p c t -> p (c t)"))
             nc.scalar.dma_start(out=out[:P, halves[half]], in_=result[:])
 
-        plain = [plain_choice(r) for r in range(2)]
-        gated = [gated_choice(0, r, halves[1]) for r in range(2)]
+        plain = plain_choice(1)
+        first_choice = gated_choice(0, 0, slice(0, T))
+        second_choice = gated_choice(0, 1, halves[1])
         first_banks = [frozen_turned([c], tag) for c, tag in enumerate(("spread", "bank0_1"))]
         second_bank = frozen_turned([2, 3], "bank0_0")
-        add_turned(gated, second_bank[:, half_chunks:, :])
-        for r in range(2):
+        for place, term in enumerate((first_choice, plain)):
             for c in range(half_chunks):
-                nc.tensor.transpose(first_banks[c][:, 1 + r, :], plain[r][:, c * P : (c + 1) * P], ident[:])
-        upper = [frozen_upright(0, "bank1_0")]
+                nc.tensor.transpose(first_banks[c][:, 1 + place, :], term[:, c * P : (c + 1) * P], ident[:])
+        add_turned([first_choice[:, halves[1]], second_choice], second_bank[:, half_chunks:, :])
+        upper = [frozen_upright(0, "bank1_1")]
 
-        second_sb = keep.tile([P, T], F32, name="second_sb")
-        nc.scalar.copy(out=second_sb[:], in_=second_bank[:].rearrange("p c t -> p (c t)"))
         first_sb = keep.tile([P, 3, T // 2], F32, name="first_sb")
         for c in range(half_chunks):
             columns = slice(c * P, (c + 1) * P)
-            nc.scalar.copy(out=first_sb[:, 0, columns], in_=first_banks[c][:, 0, :])
-            for r in range(2):
-                nc.scalar.activation(
-                    out=first_sb[:, 1 + r, columns],
-                    in_=first_banks[c][:, 1 + r, :],
-                    func=COPY,
-                    scale=gate_columns[:, r * CHUNKS + c : r * CHUNKS + c + 1],
-                )
-        finish_lower(1, [second_sb[:, tokens] for tokens in halves])
+            nc.scalar.copy(out=first_sb[:, :2, columns], in_=first_banks[c][:, :2, :])
+            nc.scalar.activation(
+                out=first_sb[:, 2, columns],
+                in_=first_banks[c][:, 2, :],
+                func=COPY,
+                scale=gate_columns[:, CHUNKS + c : CHUNKS + c + 1],
+            )
+        second_sb = keep.tile([P, T], F32, name="second_sb")
+        nc.scalar.copy(out=second_sb[:], in_=second_bank[:].rearrange("p c t -> p (c t)"))
         finish_lower(0, [first_sb[:, term, :] for term in range(3)])
-        upper.append(frozen_upright(1, "bank0_1"))
+        finish_lower(1, [second_sb[:, tokens] for tokens in halves])
+        upper.append(frozen_upright(1, "bank0_0"))
 
         choice = gated_choice(1, 0, slice(0, T))
         others = [gated_choice(1, 1, tokens) for tokens in halves]

@@ -343,16 +343,19 @@ def tile_moe_adp_gelu_kernel(
             nc.scalar.dma_start(out=out[:P, halves[half]], in_=result[:])
 
         plain = plain_choice(1)
-        first_choice = gated_choice(0, 0, slice(0, T))
-        second_choice = gated_choice(0, 1, halves[1])
-        first_banks = [frozen_turned([c], tag) for c, tag in enumerate(("spread", "bank0_1"))]
+        both_choices = [gated_choice(0, r, halves[1]) for r in range(2)]
+        first_choice = gated_choice(0, 0, halves[0])
         second_bank = frozen_turned([2, 3], "bank0_0")
-        for place, term in enumerate((first_choice, plain)):
-            for c in range(half_chunks):
-                nc.tensor.transpose(first_banks[c][:, 1 + place, :], term[:, c * P : (c + 1) * P], ident[:])
-        add_turned([first_choice[:, halves[1]], second_choice], second_bank[:, half_chunks:, :])
+        first_banks = [frozen_turned([c], tag) for c, tag in enumerate(("spread", "bank0_1"))]
+        add_turned(both_choices, second_bank[:, half_chunks:, :])
+        for c in range(half_chunks):
+            nc.tensor.transpose(first_banks[c][:, 1, :], first_choice[:, c * P : (c + 1) * P], ident[:])
+        for c in range(half_chunks):
+            nc.tensor.transpose(first_banks[c][:, 2, :], plain[:, c * P : (c + 1) * P], ident[:])
         upper = [frozen_upright(0, "bank1_1")]
 
+        second_sb = keep.tile([P, T], F32, name="second_sb")
+        nc.scalar.copy(out=second_sb[:], in_=second_bank[:].rearrange("p c t -> p (c t)"))
         first_sb = keep.tile([P, 3, T // 2], F32, name="first_sb")
         for c in range(half_chunks):
             columns = slice(c * P, (c + 1) * P)
@@ -363,11 +366,9 @@ def tile_moe_adp_gelu_kernel(
                 func=COPY,
                 scale=gate_columns[:, CHUNKS + c : CHUNKS + c + 1],
             )
-        second_sb = keep.tile([P, T], F32, name="second_sb")
-        nc.scalar.copy(out=second_sb[:], in_=second_bank[:].rearrange("p c t -> p (c t)"))
-        finish_lower(0, [first_sb[:, term, :] for term in range(3)])
         finish_lower(1, [second_sb[:, tokens] for tokens in halves])
-        upper.append(frozen_upright(1, "bank0_0"))
+        finish_lower(0, [first_sb[:, term, :] for term in range(3)])
+        upper.append(frozen_upright(1, "bank0_1"))
 
         choice = gated_choice(1, 0, slice(0, T))
         others = [gated_choice(1, 1, tokens) for tokens in halves]

@@ -158,7 +158,10 @@ def tile_moe_adp_gelu_kernel(
                 source = raw.rearrange("p j (m u v) -> p u m j v", u=2, v=2)
                 for u, copy in enumerate((nc.vector.tensor_copy, nc.scalar.copy)):
                     grouped = work.tile([P, 2, P, PACK], BF16, name="a_grouped", align_bytes=64)
-                    copy(out=grouped[:].rearrange("p v m j -> p m j v"), in_=source[:, u])
+                    rows = P // 2 if u == 1 and e < E - 2 else P
+                    for first in range(0, P, rows):
+                        part = slice(first, first + rows)
+                        copy(out=grouped[:, :, part, :].rearrange("p v m j -> p m j v"), in_=source[:, u, part])
                     values = grouped[:].rearrange("p v m j -> p (v m j)")
                     if e == E - 1 and s == PASSES - 2:
                         a_codes = wide_codes[:, u * 2 * P : (u + 1) * 2 * P]
@@ -204,7 +207,7 @@ def tile_moe_adp_gelu_kernel(
                 start=True,
                 stop=True,
             )
-            warm_up(b_codes, b_plane, {(E - 3, 1): 1, (E - 2, 0): 1, (E - 1, 0): 2}.get((e, b), 0))
+            warm_up(b_codes, b_plane, {(E - 4, 1): 1, (E - 3, 1): 1, (E - 2, 0): 2}.get((e, b), 0))
             if place == len(group) - 1:
                 nc.scalar.copy(
                     out=y_sb[b][:, group[0] * C : (e + 1) * C],
@@ -257,6 +260,32 @@ def tile_moe_adp_gelu_kernel(
             last.append(raw)
             if b == 0:
                 spent = ring[-1] - PACK * P * 4
+                nc.sync.dma_start(pos_sb[0][:], pos1)
+                nc.sync.dma_start(pos_sb[1][:], pos2)
+        final_raw = ring[-1] - PACK * P * 4
+
+        def load_frozen(b, passes):
+            words = ring_tile([P, len(passes), P], I32)
+            source = w_words.rearrange("s p n d -> p s (n d)").bitcast(I32)
+            nc.sync.dma_start(out=words[:], in_=source[:, passes[0] : passes[-1] + 1, b * P : (b + 1) * P])
+            return [words[:, place, :] for place in range(len(passes))]
+
+        w_sb = [load_frozen(0, (0, 1)) + load_frozen(0, (2, 3)), load_frozen(1, (0, 1, 2, 3))]
+
+        def frozen_turned(shared, chunks, passes):
+            for place, c in enumerate(chunks):
+                tokens = slice(c * P, (c + 1) * P)
+                for s in passes:
+                    nc.tensor.matmul_mx(
+                        out=shared[:, place, :],
+                        lhsT=x_sb[:, s, tokens].bitcast(FP8X4),
+                        lhsT_scale=xs_sb[4 * s : P, tokens],
+                        rhs=w_sb[0][s].bitcast(FP8X4),
+                        rhs_scale=ws_sb[4 * s : P, :P],
+                        start=(s == 0 and place == 0),
+                        stop=(s == PASSES - 1 and place == len(chunks) - 1),
+                    )
+
         second_layer(E - 2, 0, weave(whole[:, :, :P], nc.vector.tensor_copy))
         woven = weave(last[0][:], nc.vector.tensor_copy, "last_woven")
         h_codes = stream.tile([P, C], U32, name="last_h_codes", offset=spent, align_bytes=256)
@@ -265,17 +294,15 @@ def tile_moe_adp_gelu_kernel(
         hidden.append((h_codes, h_plane))
         second_layer(E - 1, 0, woven)
         second_layer(E - 2, 1, weave(whole[:, :, P:], nc.scalar.copy, "last_codes"), "last_woven")
+        second_bank = psum_y.tile([P, CHUNKS, P], F32, name="shared", tag="idle")
+        first_banks = [psum_y.tile([P, CHUNKS, P], F32, name="shared", tag=tag) for tag in ("spread", "bank0_1")]
+        turned = [(second_bank, [2, 3]), (first_banks[0], [0]), (first_banks[1], [1])]
+        for shared, chunks in turned:
+            frozen_turned(shared, chunks, (0, 1))
         second_layer(E - 1, 1, weave(last[1][:], nc.vector.tensor_copy, h_bytes))
+        for shared, chunks in turned:
+            frozen_turned(shared, chunks, (2, 3))
 
-        def load_frozen(b):
-            words = ring_tile([P, PASSES, P], I32)
-            source = w_words.rearrange("s p n d -> p s (n d)").bitcast(I32)
-            nc.sync.dma_start(out=words[:], in_=source[:, :, b * P : (b + 1) * P])
-            return words
-
-        nc.sync.dma_start(pos_sb[0][:], pos1)
-        nc.sync.dma_start(pos_sb[1][:], pos2)
-        w_sb = [load_frozen(b) for b in range(BLOCKS)]
 
         halves = [slice(half * T // 2, (half + 1) * T // 2) for half in range(2)]
         half_chunks = CHUNKS // 2
@@ -283,8 +310,13 @@ def tile_moe_adp_gelu_kernel(
         def entries(r, tokens):
             return pos_sb[r][:, tokens.start // 16 : tokens.stop // 16]
 
-        def gated_choice(b, r, tokens):
-            gated = keep.tile([P, tokens.stop - tokens.start], F32, name="gated%d_%d_%d" % (b, r, tokens.start))
+        def gated_choice(b, r, tokens, held=None):
+            shape = [P, tokens.stop - tokens.start]
+            label = "gated%d_%d_%d" % (b, r, tokens.start)
+            if held is None:
+                gated = keep.tile(shape, F32, name=label)
+            else:
+                gated = stream.tile(shape, F32, name=label, offset=held, align_bytes=256)
             nc.vector.tensor_tensor(gated[:], y_sb[b][:].indirect(entries(r, tokens)), gate_sb[:, r, tokens], MULT)
             return gated[:]
 
@@ -293,28 +325,12 @@ def tile_moe_adp_gelu_kernel(
             nc.scalar.activation(out=picked[:], in_=y_sb[0][:].indirect(entries(r, halves[0])), func=COPY)
             return picked[:]
 
-        def frozen_turned(chunks, tag):
-            shared = psum_y.tile([P, CHUNKS, P], F32, name="shared", tag=tag)
-            for place, c in enumerate(chunks):
-                tokens = slice(c * P, (c + 1) * P)
-                for s in range(PASSES):
-                    nc.tensor.matmul_mx(
-                        out=shared[:, place, :],
-                        lhsT=x_sb[:, s, tokens].bitcast(FP8X4),
-                        lhsT_scale=xs_sb[4 * s : P, tokens],
-                        rhs=w_sb[0][:, s, :].bitcast(FP8X4),
-                        rhs_scale=ws_sb[4 * s : P, :P],
-                        start=(s == 0),
-                        stop=(s == PASSES - 1),
-                    )
-            return shared
-
         def frozen_upright(half, tag):
             shared = psum_y.tile([P, CHUNKS, P], F32, name="shared", tag=tag)
             for s in range(PASSES):
                 nc.tensor.matmul_mx(
                     out=shared[:, :half_chunks, :].rearrange("p c t -> p (c t)"),
-                    lhsT=w_sb[1][:, s, :].bitcast(FP8X4),
+                    lhsT=w_sb[1][s].bitcast(FP8X4),
                     lhsT_scale=ws_sb[4 * s : P, P:],
                     rhs=x_sb[:, s, halves[half]].bitcast(FP8X4),
                     rhs_scale=xs_sb[4 * s : P, halves[half]],
@@ -343,10 +359,8 @@ def tile_moe_adp_gelu_kernel(
             nc.scalar.dma_start(out=out[:P, halves[half]], in_=result[:])
 
         plain = plain_choice(1)
-        both_choices = [gated_choice(0, r, halves[1]) for r in range(2)]
-        first_choice = gated_choice(0, 0, halves[0])
-        second_bank = frozen_turned([2, 3], "bank0_0")
-        first_banks = [frozen_turned([c], tag) for c, tag in enumerate(("spread", "bank0_1"))]
+        both_choices = [gated_choice(0, r, halves[1], final_raw + r * T // 2 * 4) for r in range(2)]
+        first_choice = gated_choice(0, 0, halves[0], h_bytes)
         add_turned(both_choices, second_bank[:, half_chunks:, :])
         for c in range(half_chunks):
             nc.tensor.transpose(first_banks[c][:, 1, :], first_choice[:, c * P : (c + 1) * P], ident[:])

from contextlib import ExitStack

import concourse.mybir as mybir
from concourse.masks import make_identity

K, T, E, C, H, N = 2048, 512, 8, 128, 512, 256
FLOPS = 2 * K * N * T + 2 * E * C * (K * H + H * N)

F32 = mybir.dt.float32
BF16 = mybir.dt.bfloat16
I32 = mybir.dt.int32
U32 = mybir.dt.uint32
U16 = mybir.dt.uint16
U8 = mybir.dt.uint8
FP8X4 = mybir.dt.float8_e4m3fn_x4
MULT = mybir.AluOpType.mult
ADD = mybir.AluOpType.add
GELU = mybir.ActivationFunctionType.Gelu_apprx_tanh
COPY = mybir.ActivationFunctionType.Copy

P = 128
PACK = 4
K_PASS = P * PACK
PASSES = K // K_PASS
BLOCKS = N // P
CHUNKS = T // P
PAIR = 2 * C
RING_BYTES = 128 * 1024
LAG = 3
BANK_GROUPS = (((0, 1, 2, 3), (4, 5, 6), (7,)), ((0, 1, 2, 3), (4, 5), (6, 7)))


def tile_moe_adp_gelu_kernel(
    tc, x_words, x_scales, w_words, w_scales, wa, wb, gate, offs, pos1, pos2, out
):
    nc = tc.nc
    with ExitStack() as ctx:
        keep = ctx.enter_context(tc.tile_pool(name="keep", bufs=1))
        stream = ctx.enter_context(tc.tile_pool(name="stream", bufs=1))
        twin = ctx.enter_context(tc.tile_pool(name="twin", bufs=2))
        work = ctx.enter_context(tc.tile_pool(name="work", bufs=8))
        coded = ctx.enter_context(tc.tile_pool(name="coded", bufs=12))
        psum = ctx.enter_context(tc.psum_pool(name="psum", bufs=2))
        psum_y = ctx.enter_context(tc.psum_pool(name="psum_y", bufs=1))

        offs_sb = keep.tile([P, E * C // 16], U16, name="offs_sb")
        pos_sb = [keep.tile([P, T // 16], U16, name="pos%d_sb" % r) for r in range(2)]
        x_sb = keep.tile([P, PASSES, T], I32, name="x_sb", align_bytes=256)
        xs_sb = keep.tile([P, T], U8, name="xs_sb", align_bytes=64)
        ws_sb = keep.tile([P, N], U8, name="ws_sb", align_bytes=64)
        ident = keep.tile([P, P], F32, name="ident")
        gate_rows = keep.tile([P, P], F32, name="gate_rows")
        gate_columns = keep.tile([P, 2 * CHUNKS], F32, name="gate_columns")
        gate_sb = keep.tile([P, 2, T], F32, name="gate_sb")
        y_sb = [keep.tile([P, E * C], F32, name="y%d_sb" % b) for b in range(BLOCKS)]

        idle = psum_y.tile([P, T], F32, name="idle", tag="idle")
        wide_codes = keep.tile([P, H], U32, name="wide_codes", align_bytes=64)
        wide_plane = keep.tile([P, H], U8, name="wide_plane", align_bytes=64)
        nc.gpsimd.memset(xs_sb[:], 0)

        def bank(b, turn):
            return psum_y.tile([P, CHUNKS, P], F32, name="bank", tag="bank%d_%d" % (b, turn % 2))

        def load_scale_rows(plane, scales, q):
            nc.gpsimd.dma_start(
                out=plane[32 * q : 32 * q + 16, :].bitcast(I32),
                in_=scales[:, 4 * q : 4 * q + 4, :].bitcast(I32),
            )

        nc.sync.dma_start(out=x_sb[:], in_=x_words.rearrange("s p t d -> p s (t d)").bitcast(I32))
        nc.sync.dma_start(offs_sb[:], offs)
        for q in range(4):
            load_scale_rows(xs_sb, x_scales, q)
        nc.gpsimd.memset(gate_rows[:], 0.0)
        make_identity(nc, ident[:])
        nc.gpsimd.memset(ws_sb[:], 0)

        def gather_pair(g):
            words = twin.tile([P, PASSES, PAIR], U32, name="slot_words", align_bytes=64)
            plane = twin.tile([P, PAIR], U8, name="slot_plane", align_bytes=64)
            entries = offs_sb[:, g * PAIR // 16 : (g + 1) * PAIR // 16]
            nc.vector.tensor_copy(plane[:], xs_sb[:].indirect(entries))
            for s in range(PASSES):
                nc.vector.tensor_copy(words[:, s, :], x_sb[:, s, :].bitcast(U32).indirect(entries))
            return words, plane

        ring = [0]

        def ring_tile(shape, dtype):
            size = 4
            for extent in shape[1:]:
                size = size * extent
            start = ring[-1] if ring[-1] + size <= RING_BYTES else 0
            ring.append(start + size)
            return stream.tile(shape, dtype, name="ring%d" % len(ring), offset=start, align_bytes=256)

        def load_rows(rows):
            passes = rows.shape[0] // K_PASS
            raw = ring_tile([P, passes, PACK, rows.shape[1]], F32)
            nc.sync.dma_start(
                out=raw[:].rearrange("p s j c -> p s (j c)"),
                in_=rows.rearrange("(s p j) c -> p s (j c)", p=P, j=PACK),
            )
            return raw

        def quantize(values, pool, label, tag=None):
            width = values.shape[1] // PACK
            if tag is None:
                codes = pool.tile([P, width], U32, name=label + "_codes", align_bytes=64)
            else:
                codes = keep.tile([P, width], U32, name=label + "_codes", tag=tag, align_bytes=64)
            plane = pool.tile([P, width], U8, name=label + "_plane", align_bytes=64)
            nc.vector.quantize_mx(out=codes[:].bitcast(FP8X4), scales=plane[:], in_=values)
            return codes, plane

        def warm_up(codes, plane, passes):
            for turn in range(passes):
                nc.tensor.matmul_mx(
                    out=idle[:],
                    lhsT=codes[:, :P].bitcast(FP8X4),
                    lhsT_scale=plane[:, :P],
                    rhs=wide_codes[:].bitcast(FP8X4),
                    rhs_scale=wide_plane[:],
                    start=True,
                    stop=True,
                )

        def spent_bytes(host):
            return host.rearrange("p j c -> p (j c)")[:, H // 2 : H].bitcast(BF16)

        def activate(pre, h):
            nc.scalar.activation(
                out=h.rearrange("p (c t) -> p c t", t=PACK), in_=pre[:].rearrange("p t c -> p c t"), func=GELU
            )

        def first_layer(e, earlier):
            words, plane = gathered[e // 2]
            cols = slice((e % 2) * C, (e % 2 + 1) * C)
            pre = psum.tile([P, PACK, C], F32, name="pre", tag="sums")
            done = []

            def multiply(s, u, a_codes, a_plane):
                for v in range(2):
                    done.append((s, u, v))
                    nc.tensor.matmul_mx(
                        out=pre[:, 2 * u + v, :],
                        lhsT=a_codes[:, v * P : (v + 1) * P].bitcast(FP8X4),
                        lhsT_scale=a_plane[:, v * P : (v + 1) * P],
                        rhs=words[:, s, cols].bitcast(FP8X4),
                        rhs_scale=plane[4 * s : P, cols],
                        start=(len(done) == 1),
                        stop=(len(done) == PASSES * PACK),
                    )

            for s in range(PASSES):
                raw = load_rows(wa[e, s * K_PASS : (s + 1) * K_PASS, :])[:, 0]
                source = raw.rearrange("p j (m u v) -> p u m j v", u=2, v=2)
                for u, copy in enumerate((nc.vector.tensor_copy, nc.scalar.copy)):
                    grouped = work.tile([P, 2, P, PACK], BF16, name="a_grouped", align_bytes=64)
                    rows = P // 2 if u == 1 and e < E - 2 else P
                    for first in range(0, P, rows):
                        part = slice(first, first + rows)
                        copy(out=grouped[:, :, part, :].rearrange("p v m j -> p m j v"), in_=source[:, u, part])
                    values = grouped[:].rearrange("p v m j -> p (v m j)")
                    if e == E - 1 and s == PASSES - 2:
                        a_codes = wide_codes[:, u * 2 * P : (u + 1) * 2 * P]
                        a_plane = wide_plane[:, u * 2 * P : (u + 1) * 2 * P]
                        nc.vector.quantize_mx(out=a_codes.bitcast(FP8X4), scales=a_plane, in_=values)
                    else:
                        last = e == E - 1 and s == PASSES - 1 and u == 1
                        a_codes, a_plane = quantize(values, coded, "a", "last_codes" if last else None)
                    multiply(s, u, a_codes, a_plane)
                if e == E - 1 and s >= PASSES - 2:
                    warm_up(a_codes, a_plane, (0, 0)[s - PASSES + 2])
                if e > 0 and s == 0:
                    activate(earlier, spent_bytes(raw))
                    hidden.append(quantize(spent_bytes(raw), keep, "h%d" % e))
            return pre

        def weave(raw, copy, held=None):
            if held is None:
                grouped = work.tile([P, P, PACK], BF16, name="b_grouped", align_bytes=64)
            elif isinstance(held, int):
                grouped = stream.tile([P, P, PACK], BF16, name="last_woven", offset=held, align_bytes=256)
            else:
                grouped = keep.tile([P, P, PACK], BF16, name="b_grouped", tag=held, align_bytes=64)
            copy(
                out=grouped[:].rearrange("p (c i) j -> p c j i", i=4),
                in_=raw.rearrange("p j (c i) -> p c j i", i=4),
            )
            return grouped[:].rearrange("p c j -> p (c j)")

        def second_layer(e, b, woven, held=None):
            h_codes, h_plane = hidden[e]
            turn, group = [(i, g) for i, g in enumerate(BANK_GROUPS[b]) if e in g][0]
            place = group.index(e)
            b_codes, b_plane = quantize(woven, work, "b", held)
            if place == 0:
                y_ps[b] = bank(b, turn)
            nc.tensor.matmul_mx(
                out=y_ps[b][:, place, :],
                lhsT=b_codes[:].bitcast(FP8X4),
                lhsT_scale=b_plane[:],
                rhs=h_codes[:, :].bitcast(FP8X4),
                rhs_scale=h_plane[:, :],
                start=True,
                stop=True,
            )
            warm_up(b_codes, b_plane, {(E - 4, 1): 1, (E - 3, 1): 1, (E - 2, 0): 2}.get((e, b), 0))
            if place == len(group) - 1:
                nc.scalar.copy(
                    out=y_sb[b][:, group[0] * C : (e + 1) * C],
                    in_=y_ps[b][:, : len(group), :].rearrange("p a c -> p (a c)"),
                )

        def second_layer_whole(e):
            raw = load_rows(wb[e])[:, 0]
            second_layer(e, 0, weave(raw[:, :, :P], nc.vector.tensor_copy))
            second_layer(e, 1, weave(raw[:, :, P:], nc.scalar.copy))

        def spread_gates():
            step = CHUNKS * T * 8 - T + P
            flat = gate.rearrange("r p t -> (r p t)")[3 * T : 3 * T + 2 * CHUNKS * step]
            nc.sync.dma_start(out=gate_rows[: 2 * CHUNKS, :], in_=flat.rearrange("(m s) -> m s", s=step)[:, :P])
            upright = psum_y.tile([P, P], F32, name="upright", tag="spread")
            nc.tensor.transpose(upright[:], gate_rows[:], ident[:])
            nc.scalar.copy(out=gate_columns[:], in_=upright[:, : 2 * CHUNKS])
            for r in range(2):
                spread = psum_y.tile([P, CHUNKS, P], F32, name="spread", tag="spread")
                for c in range(CHUNKS):
                    column = gate_columns[:, r * CHUNKS + c : r * CHUNKS + c + 1]
                    nc.tensor.transpose(spread[:, c, :], column.to_broadcast([P, P]), ident[:])
                nc.scalar.copy(out=gate_sb[:, r, :], in_=spread[:].rearrange("p c t -> p (c t)"))

        gathered = []
        hidden = []
        pre = None
        y_ps = [None] * BLOCKS
        for e in range(E):
            if e % 2 == 0:
                gathered.append(gather_pair(e // 2))
            pre = first_layer(e, pre)
            if e == 0:
                for q in range(4):
                    load_scale_rows(ws_sb, w_scales, q)
            if e == 1:
                spread_gates()
            if e >= LAG:
                second_layer_whole(e - LAG)
        second_layer_whole(E - 3)
        h_bytes = ring[-1] - PACK * N * 4
        last_h = stream.tile([P, H], BF16, name="last_h", offset=h_bytes, align_bytes=256)
        activate(pre, last_h[:])
        whole = load_rows(wb[E - 2])[:, 0]
        last = []
        for b in range(BLOCKS):
            raw = ring_tile([P, PACK, P], F32)
            nc.sync.dma_start(out=raw[:], in_=wb[E - 1, :, b * P : (b + 1) * P].rearrange("(p j) c -> p j c", j=PACK))
            last.append(raw)
            if b == 0:
                spent = ring[-1] - PACK * P * 4
                nc.sync.dma_start(pos_sb[0][:], pos1)
                nc.sync.dma_start(pos_sb[1][:], pos2)
        final_raw = ring[-1] - PACK * P * 4

        def load_frozen(b, passes):
            words = ring_tile([P, len(passes), P], I32)
            source = w_words.rearrange("s p n d -> p s (n d)").bitcast(I32)
            nc.sync.dma_start(out=words[:], in_=source[:, passes[0] : passes[-1] + 1, b * P : (b + 1) * P])
            return [words[:, place, :] for place in range(len(passes))]

        w_sb = [load_frozen(0, (0, 1)) + load_frozen(0, (2, 3)), load_frozen(1, (0, 1, 2, 3))]

        def frozen_turned(shared, chunks, passes):
            for place, c in enumerate(chunks):
                tokens = slice(c * P, (c + 1) * P)
                for s in passes:
                    nc.tensor.matmul_mx(
                        out=shared[:, place, :],
                        lhsT=x_sb[:, s, tokens].bitcast(FP8X4),
                        lhsT_scale=xs_sb[4 * s : P, tokens],
                        rhs=w_sb[0][s].bitcast(FP8X4),
                        rhs_scale=ws_sb[4 * s : P, :P],
                        start=(s == 0 and place == 0),
                        stop=(s == PASSES - 1 and place == len(chunks) - 1),
                    )

        second_layer(E - 2, 0, weave(whole[:, :, :P], nc.vector.tensor_copy))
        woven = weave(last[0][:], nc.vector.tensor_copy, "last_woven")
        h_codes = stream.tile([P, C], U32, name="last_h_codes", offset=spent, align_bytes=256)
        h_plane = keep.tile([P, C], U8, name="last_h_plane", align_bytes=64)
        nc.vector.quantize_mx(out=h_codes[:].bitcast(FP8X4), scales=h_plane[:], in_=last_h[:])
        hidden.append((h_codes, h_plane))
        second_layer(E - 1, 0, woven)
        second_layer(E - 2, 1, weave(whole[:, :, P:], nc.scalar.copy, "last_codes"), "last_woven")
        second_bank = psum_y.tile([P, CHUNKS, P], F32, name="shared", tag="idle")
        first_banks = [psum_y.tile([P, CHUNKS, P], F32, name="shared", tag=tag) for tag in ("spread", "bank0_1")]
        turned = [(second_bank, [2, 3]), (first_banks[0], [0]), (first_banks[1], [1])]
        for shared, chunks in turned:
            frozen_turned(shared, chunks, (0, 1))
        second_layer(E - 1, 1, weave(last[1][:], nc.vector.tensor_copy, h_bytes))
        for shared, chunks in turned:
            frozen_turned(shared, chunks, (2, 3))


        halves = [slice(half * T // 2, (half + 1) * T // 2) for half in range(2)]
        half_chunks = CHUNKS // 2

        def entries(r, tokens):
            return pos_sb[r][:, tokens.start // 16 : tokens.stop // 16]

        def gated_choice(b, r, tokens, held=None):
            shape = [P, tokens.stop - tokens.start]
            label = "gated%d_%d_%d" % (b, r, tokens.start)
            if held is None:
                gated = keep.tile(shape, F32, name=label)
            else:
                gated = stream.tile(shape, F32, name=label, offset=held, align_bytes=256)
            nc.vector.tensor_tensor(gated[:], y_sb[b][:].indirect(entries(r, tokens)), gate_sb[:, r, tokens], MULT)
            return gated[:]

        def plain_choice(r):
            picked = keep.tile([P, T // 2], F32, name="picked%d" % r)
            nc.scalar.activation(out=picked[:], in_=y_sb[0][:].indirect(entries(r, halves[0])), func=COPY)
            return picked[:]

        def frozen_upright(half, tag):
            shared = psum_y.tile([P, CHUNKS, P], F32, name="shared", tag=tag)
            for s in range(PASSES):
                nc.tensor.matmul_mx(
                    out=shared[:, :half_chunks, :].rearrange("p c t -> p (c t)"),
                    lhsT=w_sb[1][s].bitcast(FP8X4),
                    lhsT_scale=ws_sb[4 * s : P, P:],
                    rhs=x_sb[:, s, halves[half]].bitcast(FP8X4),
                    rhs_scale=xs_sb[4 * s : P, halves[half]],
                    start=(s == 0),
                    stop=(s == PASSES - 1),
                )
            return shared

        def add_turned(terms, total):
            steps = [(term, c) for c in range(half_chunks) for term in terms]
            for place, (term, c) in enumerate(steps):
                nc.tensor.matmul(
                    out=total[:, c, :],
                    lhsT=term[:, c * P : (c + 1) * P],
                    rhs=ident[:],
                    is_transpose=True,
                    start=(place == 0),
                    stop=(place == len(steps) - 1),
                )

        def finish_lower(half, terms):
            total = psum.tile([P, half_chunks, P], F32, name="total", tag="sums")
            add_turned(terms, total)
            result = keep.tile([P, T // 2], F32, name="result%d" % half, align_bytes=256)
            nc.scalar.copy(out=result[:], in_=total[:].rearrange("p c t -> p (c t)"))
            nc.scalar.dma_start(out=out[:P, halves[half]], in_=result[:])

        plain = plain_choice(1)
        both_choices = [gated_choice(0, r, halves[1], final_raw + r * T // 2 * 4) for r in range(2)]
        first_choice = gated_choice(0, 0, halves[0], h_bytes)
        add_turned(both_choices, second_bank[:, half_chunks:, :])
        for c in range(half_chunks):
            nc.tensor.transpose(first_banks[c][:, 1, :], first_choice[:, c * P : (c + 1) * P], ident[:])
        for c in range(half_chunks):
            nc.tensor.transpose(first_banks[c][:, 2, :], plain[:, c * P : (c + 1) * P], ident[:])
        upper = [frozen_upright(0, "bank1_1")]

        second_sb = keep.tile([P, T], F32, name="second_sb")
        nc.scalar.copy(out=second_sb[:], in_=second_bank[:].rearrange("p c t -> p (c t)"))
        first_sb = keep.tile([P, 3, T // 2], F32, name="first_sb")
        for c in range(half_chunks):
            columns = slice(c * P, (c + 1) * P)
            nc.scalar.copy(out=first_sb[:, :2, columns], in_=first_banks[c][:, :2, :])
            nc.scalar.activation(
                out=first_sb[:, 2, columns],
                in_=first_banks[c][:, 2, :],
                func=COPY,
                scale=gate_columns[:, CHUNKS + c : CHUNKS + c + 1],
            )
        finish_lower(1, [second_sb[:, tokens] for tokens in halves])
        finish_lower(0, [first_sb[:, term, :] for term in range(3)])
        upper.append(frozen_upright(1, "bank0_1"))

        choice = gated_choice(1, 0, slice(0, T))
        others = [gated_choice(1, 1, tokens) for tokens in halves]
        both = keep.tile([P, T], F32, name="both")
        for half, tokens in enumerate(halves):
            nc.vector.tensor_tensor(both[:, tokens], choice[:, tokens], others[half], ADD)
        for half, tokens in enumerate(halves):
            second = twin.tile([P, T // 2], F32, name="second", align_bytes=256)
            base = upper[half][:, :half_chunks, :].rearrange("p c t -> p (c t)")
            nc.vector.tensor_tensor(second[:], both[:, tokens], base, ADD)
            nc.sync.dma_start(out=out[P:, tokens], in_=second[:])
